import numpy as np, ml_dtypes
CORES = [23,119,17,113]
N = 4
import mx_ref
BF = ml_dtypes.bfloat16
def gentries(a):
    return np.ascontiguousarray(a.reshape(8, 16, -1).transpose(0, 2, 1)).reshape(8, -1)
def gtable(e):
    e = np.asarray(e); return np.ascontiguousarray(e.reshape(8, -1, 16).transpose(0, 2, 1)).reshape(128, -1).astype(np.int32)
def gcols(t, e):
    v = np.concatenate([t.reshape(8, 16, -1, 4), np.zeros((8, 16, 1, 4), BF)], axis=2)
    return np.ascontiguousarray(np.stack([v[g][:, e[g]] for g in range(8)])).reshape(128, -1)
def tile(rs):
    return np.stack(rs, axis=2).reshape(128, -1).astype(BF)
def pick(q, e):
    c = np.concatenate([q[0].reshape(128, -1, 4), np.zeros((128, 1, 4), np.uint8)], axis=1); s = np.concatenate([q[1], np.ones((16, 1), np.uint8)], axis=1)
    return (np.ascontiguousarray(c[:, e].reshape(128, -1)), np.ascontiguousarray(s[:, e]))
def join(*qs):
    return (np.concatenate([q[0] for q in qs], axis=1), np.concatenate([q[1] for q in qs], axis=1))
def put(q, e, v):
    c, s = q[0].reshape(128, -1, 4).copy(), q[1].copy(); c[:, e] = v[0].reshape(128, -1, 4); s[:, e] = v[1]
    return (c.reshape(128, -1), s)
def pk(c, s):
    return (np.ascontiguousarray(c), mx_ref.live(s))
def emit(q):
    return q[0], q[1]
def packed(v, rng):
    q = [mx_ref.quantize(np.ascontiguousarray(v[r])) for r in range(N)]
    return np.stack([a for a, b in q]), np.stack([mx_ref.plane(b, rng) for a, b in q])
def values_of_codes():
    e, c = np.zeros((128, 128, 4), np.float32), np.zeros((128, 2, 4), np.uint8)
    e[np.arange(128), np.arange(128), 0] = 1
    c[:127, :, 0] = np.arange(256).reshape(2, 128).T[:127]
    return mx_ref.matmul(mx_ref.quantize(e.reshape(128, 512).astype(BF)), (c.reshape(128, 8), np.full((16, 2), 127, np.uint8))).T.reshape(-1).astype(np.float64)
CODE_VALUE, SCALE_VALUE = values_of_codes(), 2.0 ** (np.arange(256) - 127.0)
def decode(q):
    return (CODE_VALUE[q[0]].reshape(16, 8, -1, 4) * SCALE_VALUE[q[1]][:, None, :, None] + 0.0).reshape(128, -1).astype(np.float32)
def f(rng, *shape):
    return mx_ref.flush((rng.standard_normal(shape, dtype=np.float32) * np.exp2(rng.integers(-2, 3, shape[:-1] + (1,)))).astype(BF))
def wide(rng, *shape, cols=0):
    v = rng.standard_normal(shape, dtype=np.float32) * np.exp2(rng.integers(-12, 13, shape)).astype(np.float32)
    if cols: v *= np.repeat(np.exp2(rng.integers(-cols, cols + 1, shape[:-2] + (1, shape[-1] // 4))) * (rng.random(shape[:-2] + (1, shape[-1] // 4)) > 0.0625), 4, axis=-1).astype(np.float32)
    return mx_ref.flush(v.astype(BF))
C, T, P, A = 384, 24, 8, 6
MASK = [1, 2, 3]
def numbers_of(rng):
    return {"x": np.array(f(rng, N, 128, 4 * C)), "u": np.array(f(rng, N, 128, 512)), "v": np.array(f(rng, N, 128, 512))}
def lists_of(e):
    return np.stack([gtable(e[r]) for r in range(N)])
def places(rng):
    return np.argsort(rng.random((N, 8, C)), axis=2)
def grow(rng, b):
    b[:, 0], b[:, 1] = 1, 0
    o = np.argsort(rng.random(b.shape), axis=1)
    e = np.zeros(b.shape, np.int64)
    np.put_along_axis(e, o, np.take_along_axis(o, b, axis=1), axis=1)
    return lists_of(e.reshape(N, 8, C))
def trees(rng):
    return grow(rng, rng.integers(0, np.maximum(np.arange(16), 1), (N * 8 * T, 16)))
def layers(rng):
    return np.array(f(rng, N, 128, 2048)).reshape(N, 8, 16, 4, 8, 16, 4)
def weights(rng, w, still=[]):
    for i in still:
        w[:, :, i] = 0
        w[:, :, :, :, :, i] = 0
    c, s = packed(np.ascontiguousarray(w).reshape(N, 128, 2048), rng)
    return {"wc": c, "ws": s}
def setup_inputs(rng):
    return {**numbers_of(rng), "nod": lists_of(places(rng)), "par": trees(rng), **weights(rng, layers(rng))}
def setup_inputs_ties(rng):
    d = numbers_of(rng)
    x = d["x"].reshape(N, 8, 16, C, 4)
    x[:, :, 0] = 0
    x[:, :, 0, :, 0] = rng.integers(0, 3, (N, 8, C)).astype(np.float32).astype(BF)
    u = d["u"].reshape(N, 128, 128, 4)
    u[:, :, ::16] = 0
    o = rng.permutation(N)
    for r in range(N):
        for h in range(0, 128, 16): u[r, h, h, 0] = 0.0 if r == o[0] else -1.0 if r == o[1] else 1.0
    return {"x": x.reshape(N, 128, 4 * C), "u": u.reshape(N, 128, 512), "v": d["v"], "nod": lists_of(places(rng)), "par": trees(rng), **weights(rng, layers(rng), [0])}
def setup_inputs_near(rng):
    d = numbers_of(rng)
    e = places(rng)
    o = rng.permutation(N) % 4
    x = d["x"].astype(np.float32).reshape(N, 8, 16, C, 4)
    x[:, :, 0] = 0
    x[:, :, 8:] = 0
    x[:, :, 0, :, 0] = rng.choice([-1.0, 1.0], 8)[None, :, None]
    x[:, :, 8] = ((rng.integers(0, 16, (N, 8, C))[..., None] >> np.arange(4)) & 1) * np.exp2(np.arange(4) - 23.0)
    x[:, :, 11, :, 0] = 2.0 ** -10
    u = d["u"].reshape(N, 128, 128, 4)
    u[:, :, ::16] = 0
    for r in range(N):
        k = 1.0 if o[r] == 0 else 2.0 ** -30
        if o[r] == 2:
            far = np.take_along_axis(e[r].reshape(8, T, 16), np.argsort(rng.random((8, T, 16)), axis=2)[:, :, :2], axis=2)
            x[r, :, 0] = 0
            for g in range(8):
                x[r, g, 0, far[g, :, 0], 0] = 1.0
                x[r, g, 0, far[g, :, 1], 0] = -1.0
        if o[r] == 3:
            x[r, :, 8:] = 0
            x[r, :, 10, :, 0] = rng.choice([1.0, 1.125], (8, C)) * 2.0 ** -27
        for h in range(0, 128, 16):
            if o[r] < 2:
                u[r, h, h, 0] = k
                u[r, h + 11, h, 0] = k
            if o[r] == 2: u[r, h, h, 0] = 1.0
            if o[r] < 3: u[r, h + 8, h] = k
            else: u[r, h + 10, h, 0] = k
    return {"x": x.reshape(N, 128, 4 * C).astype(BF), "u": u.reshape(N, 128, 512), "v": d["v"], "nod": lists_of(e), "par": trees(rng), **weights(rng, layers(rng), [0, 8, 9, 10, 11, 12, 13, 14, 15])}
def setup_inputs_huge(rng):
    d = numbers_of(rng)
    o = rng.permutation(N)
    h = int(np.argmin(o))
    c = rng.choice([-1.0, 1.0], (N, 1, 1, C, 1))
    c[o % 4 == 1] = -1.0
    x = (0.6 + 0.09 * rng.random((N, 8, 16, C, 4))) * c
    x[h] = 0.875 * c[h]
    x[h, 0, 0] = (0.5 + 0.375 * rng.random((C, 4))) * c[h, 0, 0]
    a = 1.0 - 0.1 * rng.random((N, 128, 8, 4))
    a[h] = 1.0
    u = d["u"].reshape(N, 128, 128, 4)
    u[:, :, ::16] = (2.0 ** 30 * a).astype(np.float32).astype(BF)
    w = np.zeros((N, 128, 4, 128, 4), np.float32)
    i = np.arange(128)
    for b in range(4): w[:, i, b, i, b] = -1
    return {"x": (2.0 ** 30 * x).astype(np.float32).reshape(N, 128, 4 * C).astype(BF), "u": u.reshape(N, 128, 512), "v": d["v"], "nod": lists_of(places(rng)), "par": trees(rng), **weights(rng, w.astype(BF))}
def setup_inputs_forms(rng):
    d = numbers_of(rng)
    x = d["x"].reshape(N, 8, 16, C, 4)
    z = (N, 8, 8, C, 4)
    n = rng.integers(8, 15, z)
    n[:, :, 1, :, 0] = (rng.permutation(8) % 7 + 8)[:, None]
    x[:, :, 8:] = ((9 + 2 * rng.integers(0, 4, z)) * np.exp2(-3.0 - n) * rng.choice([-1.0, 1.0], z)).astype(np.float32).astype(BF)
    x[:, :, 8, :, 0] = 1.96875
    i = np.arange(16)
    b = np.stack([0 * i, np.maximum(i - 1, 0), i % 2, np.where(i < 8, np.maximum(i - 1, 0), 7)])
    k = rng.integers(0, 4, (N, 8 * T))
    e = rng.permutation(N)
    k[e[0]] = 0
    k[e[1]] = 1
    u = d["u"].reshape(N, 128, 128, 4)
    for r in e[N // 2:]:
        u[r, :, ::16] = 0
        for h in range(0, 128, 16): u[r, h + 9, h, 0] = 1.0
    w = layers(rng)
    w[:, :, :, :, :, 8:] = 0
    return {"x": x.reshape(N, 128, 4 * C), "u": u.reshape(N, 128, 512), "v": d["v"], "nod": lists_of(places(rng)), "par": grow(rng, b[k.reshape(-1)]), **weights(rng, w)}
def setup_inputs_spread(rng):
    d = setup_inputs(rng)
    d["x"] = wide(rng, N, 128, 4 * C, cols=6)
    return d
def check_inputs(d):
    b = []
    for k in ("x", "u", "v"):
        a = np.abs(d[k].astype(np.float32))
        if not (np.isfinite(a).all() and ((a == 0) | (a >= 2.0 ** -30) & (a <= 2.0 ** 30)).all()): b.append("a value of " + k)
    e = np.stack([gentries(d["nod"][r]) for r in range(N)])
    if (np.sort(e, axis=2) != np.arange(C)).any(): b.append("nod: a group whose entries aren't every column once")
    e = np.stack([gentries(d["par"][r]) for r in range(N)]).reshape(-1, 16).astype(np.int64)
    i = np.arange(16)
    if ((e < 0) | (e > 15)).any(): b.append("an entry of par")
    else:
        two = (np.take_along_axis(e, e, axis=1) == i) & (e != i)
        far = e
        for j in range(4): far = np.take_along_axis(far, far, axis=1)
        if (np.count_nonzero(two, axis=1) != 2).any() or (e == i).any() or not np.take_along_axis(two, far, axis=1).all(): b.append("par: links that aren't a tree's")
    none, least, most = [emit(mx_ref.quantize(np.full((128, 16), k, np.float32).astype(BF)))[1][0, 0] for k in (0.0, 2.0 ** -30, 2.0 ** 30)]
    for r in range(N):
        if ((d["wc"][r] == 0x7F) | (d["wc"][r] == 0xFF)).any(): b.append("wc: a code that is no number")
        s = mx_ref.live(d["ws"][r])
        if ((s != none) & ((s < least) | (s > most))).any(): b.append("ws: a scale out of range")
    return b
def reference(x, u, v, nod, par, wc, ws):
    qu = [mx_ref.quantize(u[r]) for r in range(N)]
    lay = [pk(wc[r], ws[r]) for r in range(N)]
    now = [x[r] for r in range(N)]
    place = np.stack([gentries(nod[r]) for r in range(N)]).reshape(-1, 16).astype(np.int64)
    link = np.stack([gentries(par[r]) for r in range(N)]).reshape(-1, 16).astype(np.int64)
    m = np.arange(N * 8 * T)
    for mask in MASK:
        q = [mx_ref.quantize(now[r]) for r in range(N)]
        own = [decode(q[r]) for r in range(N)]
        s = np.stack([mx_ref.matmul(qu[r], q[r])[::16] for r in range(N)]) + np.float32(0.0)
        s = np.take_along_axis(s, place.reshape(N, 8, C), axis=2).reshape(-1, 16)
        o = np.argsort(-s, axis=1, kind="stable")
        st = np.argsort(o, axis=1)
        col = np.take_along_axis(place, o, axis=1)
        to = np.take_along_axis(st, link, axis=1)
        edge = np.zeros((len(m), 16, 16), bool)
        edge[m[:, None], st, to] = True
        edge[m[:, None], to, st] = True
        word = np.zeros((len(m), 14), np.int64)
        for j in range(14):
            a = np.argmax(np.count_nonzero(edge, axis=2) == 1, axis=1)
            word[:, j] = np.argmax(edge[m, a], axis=1)
            edge[m, a, word[:, j]] = False
            edge[m, word[:, j], a] = False
        give = np.take_along_axis(col, word[:, A:], axis=1).reshape(N, 8, T * P)
        sent = [mx_ref.quantize(gcols(own[r].astype(BF), give[r])) for r in range(N)]
        other = word.reshape(N, 8 * T, 14)[np.arange(N) ^ mask].reshape(-1, 14)
        c = np.concatenate([word[:, :A], other[:, A:]], axis=1)
        free = np.ones((len(m), 16), bool)
        need = np.count_nonzero(c[:, :, None] == np.arange(16), axis=1)
        to, src = np.zeros((len(m), 16), np.int64), np.zeros((len(m), 16), np.int64)
        for j in range(14):
            a = np.argmax(free & (need == 0), axis=1)
            to[m, a] = c[:, j]
            src[m, a] = col[m, c[:, j]] if j < A else C + P * (m % T) + j - A
            free[m, a] = False
            need[m, c[:, j]] -= 1
        a = np.argmax(free, axis=1)
        free[m, a] = False
        b = np.argmax(free, axis=1)
        to[m, a], to[m, b] = b, a
        src[m, a], src[m, b] = col[m, b], col[m, a]
        link = np.zeros((len(m), 16), np.int64)
        np.put_along_axis(link, o, np.take_along_axis(o, to, axis=1), axis=1)
        e = np.zeros((N, 8, C), np.int64)
        np.put_along_axis(e, col.reshape(N, 8, C), src.reshape(N, 8, C), axis=2)
        for r in range(N):
            both = np.concatenate([own[r], decode(sent[r ^ mask])], axis=1).astype(BF)
            z = ((own[r] + gcols(both, e[r]).astype(np.float32)) * np.float32(0.5)).astype(BF)
            qz = mx_ref.quantize(z)
            now[r] = tile([mx_ref.matmul(pick(lay[r], np.arange(128 * k, 128 * k + 128)), qz) * np.float32(0.03125) + z[:, k::4].astype(np.float32) for k in range(4)])
    y = np.zeros((N, 128, C), np.float32)
    oc, osc = np.zeros((N, 128, 4 * C), np.uint8), np.zeros((N, 16, C), np.uint8)
    for r in range(N):
        q = mx_ref.quantize(now[r])
        y[r] = mx_ref.matmul(mx_ref.quantize(v[r]), q)
        oc[r], osc[r] = emit(q)
    return {"y": y, "op": link.reshape(N, 8, C).astype(np.float32), "oc": oc, "osc": osc}

@@ -1,0 +1,570 @@
+from concourse.bass import DstId, RemoteDMATransfer
+from concourse.mybir import dt, AluOpType, ActivationFunctionType
+
+C = 384
+K = 24
+H = C // 2
+ROUNDS = (1, 2, 3)
+F8, U8, BF, F16, F32, I32, U16 = "float8_e4m3fn_x4", "uint8", "bfloat16", "float16", "float32", "int32", "uint16"
+SIZE = {F8: 4, U8: 1, BF: 2, F16: 2, F32: 4, I32: 4, U16: 2}
+
+SCRATCH = {}
+PLACE = {}
+
+
+def _buf(names, cols, kind):
+    for n in names.split():
+        SCRATCH[n] = ("sbuf", [128, cols], kind)
+        PLACE[n] = (n, 0, cols)
+
+
+def _pool(pool, kind, *parts):
+    at = 0
+    for names, cols in parts:
+        for n in names.split():
+            PLACE[n] = (pool, at, cols)
+            at += (cols + 15) // 16 * 16
+    SCRATCH[pool] = ("sbuf", [128, at], kind)
+
+
+_buf("x0 xt ft zt z32 x32 hn", 4 * C, BF)
+_buf("wt", 8 * C, BF)
+_buf("ut vt", 512, BF)
+_buf("et", 2048, BF)
+_buf("idn", 128, BF)
+_buf("qx qz qf0 qf1 qf2 lf0 lf1 lf2", C, F8)
+_buf("sx sz sf0 sf1 sf2 ls0 ls1 ls2", C, U8)
+_buf("qe qw", 512, F8)
+_buf("se sw", 512, U8)
+_buf("qu qur qv", 128, F8)
+_buf("su sur sv", 128, U8)
+_buf("nodi pari", K, I32)
+_buf("pidx", 8, I32)
+_buf("uli", 8, F32)
+_buf("ulu", 8, U16)
+_buf("nodu np0 np1 np2", K, U16)
+_buf("yt opn", C, F32)
+_buf("w1s0 w1s1 w1s2 w1l0 w1l1 w1l2", K, BF)
+_buf("w2s0 w2s1 w2s2 w2l0 w2l1 w2l2", 2 * K, BF)
+_pool("lf32", F32, ("cols ge lt", 16), ("iota srcw", 2 * C), ("cs ownsl osl", 2 * K),
+      ("k16 k256 cg0 stc st16 siz8 vm ownm owng cg key " + " ".join("t%d" % i for i in range(14)), K),
+      ("nodnr sc s1 f1 f2 inv1 inv2 selw", C))
+_pool("lu16", U16, ("c15 d2u invu stu g0 g1 g2 g4 g8 keyu o3u o3q ogu cgu of2 srcu", K), ("oslu", 2 * K))
+_pool("lbf", BF, ("selg jt16 dji diag dpm keep thr keepl selm hd1 zero d2 d4 d8 db c2 c4 c8 pa pb pc pd sel0 siz sell "
+                  "dif cmpm cm2 tmp stn stl xx mx mn spk spc nbk nbc cmk pos g3c g3q wc1 wq eq seen asum won lk lsc "
+                  "yq hh stsc", C),
+      ("jw wdec", 912), ("valt valm tw3 tw2", 256), ("ktab", 544), ("xtab", 16), ("ab", C + 16))
+_pool("lf16", F16, ("h2 h4 h8 oh osum src1 src2", C))
+SCRATCH["ps"] = ("psum", [128, 4096], F32)
+PLACE["ps"] = ("ps", 0, 4096)
+
+LOADS = ["dx", "dnod", "dpar", "du", "dwc", "dws", "dv"]
+SEMAPHORES = (["qV", "qS", "qP", "qG", "sent", "stored"] + LOADS
+              + ["%s%d" % (n, r) for n in ("an", "af", "as", "aw", "ax") for r in range(3)])
+
+Alu = AluOpType
+Act = ActivationFunctionType
+TUNE = dict(word=3.0, big=6.0, wake=0.07, iss=0.02, look=0.3, seed=3, noise=3.0, turns=1200, moves=6)
+ORDER = {}
+
+
+def _meet(a, b):
+    if a[0] >= b[1] or b[0] >= a[1]:
+        return False
+    return a[2] != b[2] or (a[0] - b[0]) % a[2] == 0
+
+
+def _order(ops, queues):
+    n = len(ops)
+    before = [sorted(o["need"]) for o in ops]
+    after = [[] for _ in ops]
+    for i in range(n):
+        for j in before[i]:
+            after[j].append(i)
+    cost = [o["cost"] + TUNE["iss"] for o in ops]
+
+    def lag(i, j):
+        return 0.0 if ops[i]["q"] == ops[j]["q"] == "P" else ops[i]["late"] + TUNE["wake"]
+
+    def lay(rank_):
+        left = [len(p) for p in before]
+        ready = [0.0] * n
+        free = {q: 0.0 for q in queues}
+        mine = {q: [i for i in range(n) if not left[i] and ops[i]["q"] == q] for q in queues}
+        at = [0.0] * n
+        for _ in range(n):
+            best = None
+            for q, m in mine.items():
+                if m:
+                    t = max(free[q], min(ready[i] for i in m))
+                    i = min((i for i in m if ready[i] <= t + 0.02), key=lambda i: rank_[i])
+                    soon = [j for j in m if rank_[j] < rank_[i] and ready[j] < t + TUNE["look"] * cost[i]]
+                    if soon:
+                        i = min(soon, key=lambda j: rank_[j])
+                    s = max(free[q], ready[i])
+                    if best is None or s < best[0]:
+                        best = (s, i)
+            s, i = best
+            at[i] = s
+            free[ops[i]["q"]] = s + cost[i]
+            mine[ops[i]["q"]].remove(i)
+            for j in after[i]:
+                ready[j] = max(ready[j], s + cost[i] + lag(i, j))
+                left[j] -= 1
+                if not left[j]:
+                    mine[ops[j]["q"]].append(j)
+        return at
+
+    way = [0.0] * n
+    for i in range(n - 1, -1, -1):
+        way[i] = cost[i] + max([way[j] + lag(i, j) for j in after[i]] + [ops[i]["late"]])
+    seed = [TUNE["seed"]]
+
+    def draw():
+        seed[0] = (seed[0] * 6364136223846793005 + 1442695040888963407) % 2 ** 64
+        return (seed[0] >> 33) / 2.0 ** 31
+
+    rank_, best = [-w for w in way], None
+    for turn in range(TUNE["turns"]):
+        new = list(rank_)
+        if turn:
+            for _ in range(TUNE["moves"]):
+                i, d = int(draw() * n), TUNE["noise"] * (draw() - 0.5)
+                for j in [i] + (before[i] if d < 0 else after[i]):
+                    new[j] += d
+        at = lay(new)
+        end = max(at[i] + cost[i] + ops[i]["late"] for i in range(n))
+        if best is None or end <= best[0]:
+            best, rank_ = (end, at), new
+    ORDER["end"] = best[0]
+    return sorted(range(n), key=lambda i: (best[1][i], i))
+
+
+def rank_program(g, core, T, topo):
+    rank = T.rank_of(core)
+    if rank is None:
+        return
+    eng = {"V": g.vector, "S": g.scalar, "P": g.tensor, "G": g, "Y": g.sync}
+    ops = []
+    acc = {}
+
+    def v(name, a=0, b=None, s=1):
+        buf, at, n = PLACE[name]
+        a, b = at + a, at + (n if b is None else b)
+        ap = T[buf][:, a:b] if s == 1 else T[buf][:, a:b:s]
+        run_ = (a // 512 * 512, (b + 511) // 512 * 512, 1) if buf == "ps" else (a, b, s)
+        return (ap, [(buf, run_)], len(range(a, b, s)), SIZE[SCRATCH[buf][2]], False)
+
+    def last(name):
+        return v(name, 15, C, 16)
+
+    def first(name):
+        return v(name, 0, C, 16)
+
+    def col(j, name="cols"):
+        return v(name, j, j + 1)
+
+    def ind(win, off):
+        return (win[0].indirect(off[0]), win[1] + off[1], 16 * off[2], win[3], True)
+
+    def bits(x, kind):
+        return (x[0].bitcast(kind),) + x[1:]
+
+    def add(q, issue, reads, writes, cost, late=0.0, sem=None, inc=1):
+        need = set()
+        for w, rs in ((False, reads), (True, writes)):
+            for name, run_ in rs:
+                for a in acc.get(name, []):
+                    if (w or a[1] or (name == "ps" and a[2] != q)) and _meet(run_, a[0]):
+                        need.add(a[3])
+        me = len(ops)
+        ops.append(dict(q=q, issue=issue, need=need, cost=cost, late=late, sem=sem or "q" + q, inc=inc))
+        for name, r_ in writes:
+            acc[name] = [a for a in acc.get(name, []) if not (
+                r_[0] <= a[0][0] and a[0][1] <= r_[1] and (r_[2] == 1 or (r_[2] == a[0][2] and _meet(r_, a[0]))))]
+            acc[name].append((r_, True, q, me))
+        for name, r_ in reads:
+            acc.setdefault(name, []).append((r_, False, q, me))
+
+    def run(q, fn, out, args, cost, kw=None, more=(), reads=()):
+        kw = kw or {}
+        rd = [r for a in list(args) + list(kw.values()) + list(reads) if isinstance(a, tuple) for r in a[1]]
+        wr = list(out[1]) + [r for a in more for r in a[1]]
+        pick = lambda a: a[0] if isinstance(a, tuple) else a
+        add(q, lambda: fn(out[0], *[a[0] for a in more], *[pick(a) for a in args], **{k: pick(a) for k, a in kw.items()}),
+            rd, wr, cost)
+
+    def plain(a, per):
+        return 0.055 + a[2] * 0.0013 if a[4] else max(64, a[2] * per) * 0.001
+
+    def half(*xs):
+        return 0.5 if all(x[3] == 2 for x in xs) else 1
+
+    def tt(out, a, b, op):
+        run("V", g.vector.tensor_tensor, out, [a, b, op], plain(a, 1 if a[1][0][0] == "ps" else 2 * half(out, a, b)))
+
+    def ts(out, a, s1, op0, s2=None, op1=None):
+        run("V", g.vector.tensor_scalar, out, [a, s1, s2, op0] + ([] if op1 is None else [op1]), plain(a, half(out, a)))
+
+    def cp(out, a):
+        run("V", g.vector.tensor_copy, out, [a], plain(a, half(out, a)))
+
+    def scan(out, d0, d1, op0, op1):
+        run("V", g.vector.tensor_tensor_scan, out, [d0, d1, 0.0, op0, op1], plain(out, half(out, d0, d1)))
+
+    def total(out, d):
+        scan(out, v("keep"), d, Alu.mult, Alu.add)
+
+    def fill(out, c):
+        run("V", g.vector.memset, out, [c], plain(out, half(out)))
+
+    def quant(q, s, a):
+        run("V", g.vector.quantize_mx, q, [a], 0.015 + 0.00028 * a[2], more=[s])
+
+    def act(out, a, scale=1.0, bias=None, func=None):
+        kw = {} if scale == 1.0 else {"scale": scale}
+        if bias is not None:
+            kw["bias"] = bias
+        if func is None:
+            func = Act.Copy if bias is None and not isinstance(scale, tuple) else Act.Identity
+        run("S", g.scalar.activation, out, [a, func], plain(a, 1), kw)
+
+    def gather(out, a, win, off):
+        act(v(out, a + H, a + C), ind(win, v(off, K // 2, K)))
+        cp(v(out, a, a + H), ind(win, v(off, 0, K // 2)))
+
+    def bank(b, n=C):
+        return v("ps", 512 * b, 512 * b + n)
+
+    def mm(at, w, ws, b, x, xs, a=0, n=C):
+        run("P", g.tensor.matmul_mx, bank(at, n),
+            [v(w, 128 * b, 128 * b + 128), v(ws, 128 * b, 128 * b + 128), v(x, a, a + n), v(xs, a, a + n), True, True],
+            (n + 16) * 0.0006)
+
+    def iota(out, pattern, base=0, mult=0, small=True):
+        run("G", g.iota, out, [pattern, base, mult], 0.13 + 0.002 * out[2],
+            {"allow_small_or_imprecise_dtypes": True} if small else {})
+
+    def load(q, sem, out, src, late):
+        add(q, lambda: eng[q].dma_start(out[0], src), [], out[1], 0.05, late, sem, 16)
+
+    def store(q, dst, ap, reads):
+        add(q, lambda: eng[q].dma_start(dst, ap), reads, [], 0.05, 2.5, "stored", 16)
+
+    def peer(r):
+        return T.cores[rank ^ ROUNDS[r]]
+
+    sent = [0]
+
+    def send(dst, land, src, sem, part, late):
+        e = topo.engines(core, dst)
+        n = len(e) // 2
+        m = sum(1 << k for k in e[part * n:(part + 1) * n])
+        rid, pid, _ = topo.addr(dst)
+        sent[0] += n
+        add("G", lambda: g.remote_dma(land[0], src[0], T.sem[sem], T.sem.sent, pid, rid, m), src[1], land[1], 0.3, late,
+            (sem,), n)
+
+    PM, CA, CB, ST, O3, MQ, ML, I16, MUT, ST4, GL, T0, T1, T2, T3, T4 = range(16)
+    GE6, GE14, E15, LT6, LT15 = col(6, "ge"), col(14, "ge"), col(15, "ge"), col(6, "lt"), col(15, "lt")
+
+    load("Y", "dx", v("x0"), T.x[:], 3.2)
+    load("S", "dnod", v("nodi"), T.nod[:], 2.1)
+    load("S", "dpar", v("pari"), T.par[:], 2.1)
+    load("S", "du", v("ut"), T.u[:], 2.6)
+    load("Y", "dwc", bits(v("qw"), dt.uint8), T.wc[:], 4.0)
+    load("Y", "dws", v("sw"), T.ws[:], 4.0)
+    load("Y", "dv", v("vt"), T.v[:], 4.0)
+
+    jt = v("jw", 0, C)
+    iota(v("pidx", 0, 1), [[0, 1]], 0, 1, False)
+    iota(jt, [[0, K], [1, 16]])
+    iota(v("k16"), [[16, K]])
+    iota(v("uli"), [[16, 8]])
+    iota(v("idn"), [[1, 128]], 0, -1)
+    iota(v("iota"), [[1, 2 * C]])
+    iota(v("valt"), [[1, 16], [0, 16]])
+    iota(v("selg"), [[256, K], [0, 16]], 256)
+    ts(v("pidx", 1, 2), v("pidx", 0, 1), 15, Alu.bitwise_and)
+    cp(col(PM), v("pidx", 1, 2))
+    ts(v("ge"), v("jw", 0, 16), col(PM), Alu.is_le)
+    ts(v("lt"), v("jw", 0, 16), col(PM), Alu.is_gt)
+    ts(v("dji"), jt, col(PM), Alu.subtract)
+    act(col(I16), col(PM), 16.0)
+    act(col(ST), LT15, 256.0)
+    act(col(ST4), LT15, 1024.0)
+    act(col(O3), LT15, 256.0, 4096.0)
+    act(col(CB), LT15, 1.0, 14.0)
+    act(col(T0), LT15, 2.0, -1.0)
+    act(col(CA), col(PM), 1.0, col(T0))
+    act(col(MUT), col(I16), 1.0, col(ST))
+    act(col(MQ), GE14, -1.0, GE6)
+    act(col(ML), E15, -1.0, GE6)
+    act(col(T1), col(MQ), 384.0)
+    act(col(T2), E15, 15.0)
+    act(col(T3), E15, 512.0)
+    act(col(GL), col(1, "lt"), 8192.0, -256.0)
+    act(v("cs", 0, K), v("k16"), 1.0, col(T1))
+    act(v("cs", K, 2 * K), v("k16"), 1.0, col(T2))
+    act(v("cg0"), v("k16"), 1.0, col(T3))
+    act(v("jt16"), jt, 16.0)
+    act(v("k256"), v("k16"), 16.0)
+    ts(v("diag"), v("dji"), 0.0, Alu.is_equal)
+    ts(v("keep"), jt, 1.0, Alu.min)
+    act(v("dpm"), v("diag", 0, 256) if False else v("diag"), 2.0, -1.0)
+    act(v("hd1"), v("diag"), 0.5, -1.0)
+    act(v("eq"), v("diag"), -1024.0)
+    ts(v("seen"), v("dji"), 1.0, Alu.is_equal, 256.0, Alu.mult)
+    tt(v("selm"), v("eq"), v("seen"), Alu.add)
+    act(v("selw"), v("selm"), 4.0)
+    tt(v("selg"), v("selg"), v("diag"), Alu.mult)
+    ts(v("tmp"), v("dji"), -1.0, Alu.is_equal, -8192.0, Alu.mult)
+    ts(last("tmp"), last("dji"), 15.0, Alu.is_equal, -8192.0, Alu.mult)
+    tt(v("selg"), v("selg"), v("tmp"), Alu.add)
+    ts(v("c15"), v("k16"), 15.0, Alu.add)
+    ts(v("thr"), v("dji"), 0.0, Alu.is_lt, 2.0 ** -110, Alu.mult)
+    act(v("xtab"), v("iota", 0, 16), 256.0, 256.0)
+    act(v("ktab"), v("iota", 0, 544), 16.0, -4224.0, Act.Abs)
+    ts(v("tw3"), v("jw", 0, 256), col(CA), Alu.is_equal)
+    ts(v("valm"), v("valt"), col(CB), Alu.min)
+    tt(v("tw3"), v("tw3"), v("valm"), Alu.mult)
+    ts(v("tw2"), v("valt"), col(PM), Alu.is_equal, 2.0, Alu.mult)
+    ts(v("tw2"), v("tw2"), -1.0, Alu.add)
+    tt(v("tw2"), v("tw2"), v("dpm", 0, 256), Alu.max)
+    act(v("spk"), jt, 0.0)
+    act(v("spc"), jt, 0.0)
+    act(v("zero"), jt, 0.0)
+    act(v("jw", C), v("iota", 0, 912 - C), 0.0, 31.0)
+    act(v("wdec", C), v("iota", 0, 912 - C), 0.0, -1.0)
+    ts(v("keepl"), v("dji"), 1.0, Alu.not_equal)
+    act(last("keepl"), last("keepl"), 512.0)
+    act(first("keepl"), first("keepl"), 0.0)
+    fill(v("et"), 0.0)
+    for b in range(4):
+        ts(v("et", 512 * b + b, 512 * (b + 1), 4), v("idn"), 0.0, Alu.is_equal)
+    quant(v("qe"), v("se"), v("et"))
+    cp(v("ulu"), v("uli"))
+    quant(v("qu"), v("su"), v("ut"))
+    cp(bits(v("qur"), dt.uint32), ind(bits(v("qu"), dt.uint32), v("ulu")))
+    act(v("sur"), ind(v("su"), v("ulu")))
+    quant(v("qv"), v("sv"), v("vt"))
+
+    def glob(out, tmp, loc):
+        tt(v(tmp), loc, v("k256"), Alu.add)
+        ts(v(out), v(tmp), 0.0625, Alu.mult)
+
+    def diagonal(out, x, hold="selm"):
+        scan(out, v(hold), x, Alu.add, Alu.max)
+
+    def places(out, tmp, x):
+        scan(v(tmp), v(x), v("selg"), Alu.max, Alu.add)
+        ts(v(out), last(tmp), col(GL), Alu.add, 0.0625, Alu.mult)
+
+    cp(v("nodu"), v("nodi"))
+    moves = []
+    e = [k for k in topo.engines(core, peer(0)) if all(k in topo.engines(core, peer(j)) for j in range(3))]
+    n = len(e) // 4
+    for r in range(3):
+        rid, pid, _ = topo.addr(peer(r))
+        moves.append(RemoteDMATransfer(dst_ids=[DstId(rid=rid, pnc=pid)], remote_sem=T.sem["an%d" % r],
+                                       dma_engine_mask=sum(1 << k for k in e[r * n:(r + 1) * n]),
+                                       src=T.nodu[:], dst=T["np%d" % r][:]))
+    sent[0] += 3 * n
+    add("G", lambda: g.remote_dma_fused(moves, local_sem=T.sem.sent), v("nodu")[1],
+        v("np0")[1] + v("np1")[1] + v("np2")[1], 2.0, 4.0, ("an0", "an1", "an2"), n)
+    act(v("nodnr"), ind(v("iota", 0, C), v("nodu")))
+    run("V", g.vector.tensor_copy, (ind(v("inv1"), v("nodu"))[0], v("inv1")[1]), [v("iota", 0, C)], 1.3, reads=[v("nodu")])
+    diagonal(v("inv2"), v("inv1"), "selw")
+    ts(v("invu"), last("inv2"), col(ST4), Alu.subtract)
+
+    ts(last("lsc"), v("pari"), 16.0, Alu.mult)
+    glob("g0", "t0", last("lsc"))
+    act(v("pc"), ind(v("jt16"), v("g0")))
+    act(v("pd"), ind(v("pc"), v("g0")))
+    ts(v("t1"), last("lsc"), col(I16), Alu.is_gt)
+    ts(v("t2"), last("lsc"), -1.0, Alu.mult, col(I16), Alu.add)
+    tt(v("t1"), v("t1"), v("t2"), Alu.mult)
+    diagonal(v("sel0"), v("pd"))
+    ts(v("t3"), last("sel0"), col(MUT), Alu.is_equal)
+    tt(v("t1"), v("t1"), v("t3"), Alu.mult)
+    tt(last("lsc"), last("lsc"), v("t1"), Alu.add)
+    glob("g1", "t0", last("lsc"))
+    quant(v("qx"), v("sx"), v("x0"))
+
+    for r in range(3):
+        to = peer(r)
+        final = r == 2
+        qf, sf, lf, ls = ("qf%d" % r, "sf%d" % r, "lf%d" % r, "ls%d" % r)
+        w1s, w1l, w2s, w2l = ("w1s%d" % r, "w1l%d" % r, "w2s%d" % r, "w2l%d" % r)
+        act(v("pa"), ind(v("jt16"), v("g1")))
+        act(v("pb"), ind(v("pa"), v("g1")))
+        ts(v("d2u"), last("lsc"), col(PM), Alu.add)
+        act(v("d2"), ind(v("tw2"), v("d2u")))
+        cp(v("c2"), v("d2"))
+        places("g2", "h2", "pb")
+        act(v("pc"), ind(v("pb"), v("g2")))
+        tt(v("d4"), ind(v("d2"), v("g2")), v("c2"), Alu.max)
+        act(v("c4"), v("d4"))
+        places("g4", "h4", "pc")
+        act(v("pd"), ind(v("pc"), v("g4")))
+        tt(v("d8"), ind(v("d4"), v("g4")), v("c4"), Alu.max)
+        act(v("c8"), v("d8"))
+        places("g8", "h8", "pd")
+        tt(v("db"), ind(v("d8"), v("g8")), v("c8"), Alu.max)
+        total(v("siz"), v("db"))
+        act(v("siz8"), last("siz"), 8.0)
+        mm(4, "qur", "sur", 0, "qx", "sx")
+        act(v("sc"), bank(4))
+        for b in range(4):
+            mm(b, "qe", "se", b, "qx", "sx")
+        act(v("s1"), ind(v("sc"), v("nodu")))
+        tt(v("f1"), ind(v("sc"), v("nodu")), v("diag"), Alu.mult)
+        total(v("f2"), v("f1"))
+        tt(v("dif"), ind(v("f2"), v("c15")), v("s1"), Alu.subtract)
+        tt(v("cmpm"), v("dif"), v("thr"), Alu.is_lt)
+        total(v("stsc"), v("cmpm"))
+        ts(v("stu"), last("stsc"), 0.0, Alu.add)
+        act(v("stn"), ind(v("jt16", 0, 16), v("stu")))
+        act(v("stl"), ind(v("stn"), v("g1")))
+        act(v("st16"), last("stsc"), 16.0, col(ST))
+        act(v("stc"), last("stsc"), 1.0, -16.5)
+        for b in range(4):
+            act(v("ft", b, 4 * C, 4), bank(b))
+        quant(v(qf), v(sf), v("ft"))
+        send(to, bits(v(lf), dt.uint8), bits(v(qf), dt.uint8), "af%d" % r, 0, TUNE["big"])
+        send(to, v(ls), v(sf), "as%d" % r, 0, TUNE["big"])
+        for b in range(4):
+            act(v("wt", 2 * C * b, 2 * C * b + C), bank(b), 0.5)
+        act(v("srcw", C, 2 * C), ind(v("iota", C, 2 * C), v("np%d" % r)))
+        tt(v("xx"), ind(v("xtab"), v("stu")), v("db"), Alu.mult)
+        scan(v("mx"), v("keep"), v("xx"), Alu.mult, Alu.max)
+        scan(v("mn"), v("keep"), v("xx"), Alu.mult, Alu.min)
+        tt(v("t4"), last("mx"), v("siz8"), Alu.add)
+        tt(v("key"), v("t4"), last("mn"), Alu.add)
+        act(first("spk"), v("key"), func=Act.Abs)
+        ts(v("keyu"), v("key"), 0.0625, Alu.mult, 264.0, Alu.add)
+        total(v("nbk"), v("spk"))
+        tt(v("cmk"), ind(v("ktab"), v("keyu")), v("nbk"), Alu.is_gt)
+        total(v("pos"), v("cmk"))
+        diagonal(v("sell"), v("stl"))
+        tt(v("t5"), last("mx"), v("st16"), Alu.add)
+        tt(v("t6"), last("sell"), last("mn"), Alu.subtract)
+        tt(v("vm"), v("t5"), v("t6"), Alu.max)
+        tt(v("t7"), v("vm"), last("pos"), Alu.add)
+        ts(v("o3u"), v("t7"), col(O3), Alu.subtract)
+        gather("g3c", 0, v("tw3"), "o3u")
+        total(v("wc1"), v("g3c"))
+        ts(v(w1s), last("wc1"), GE6, Alu.mult)
+        send(to, v(w1l), v(w1s), "aw%d" % r, 1, TUNE["word"])
+        act(v("t8"), last("mx"), 1.0, col(I16))
+        tt(v("t9"), last("lsc"), last("mn"), Alu.subtract)
+        tt(v("t9"), v("t8"), v("t9"), Alu.max)
+        tt(v("t9"), v("t9"), last("pos"), Alu.add)
+        ts(v("o3q"), v("t9"), 4096.0, Alu.subtract)
+        act(v("g3q"), ind(v("tw3"), v("o3q")))
+        total(v("wq"), v("g3q"))
+        act(v("t10"), last("wc1"), GE14)
+        act(v("t11"), last("wq"), col(MQ))
+        act(v(w2s, K, 2 * K), last("wc1"), GE6 if final else col(ML))
+        tt(v(w2s, 0, K), v("t10"), v("t11"), Alu.add)
+        send(to, v(w2l), v(w2s), "ax%d" % r, 1, TUNE["word"])
+        tt(v("oh"), ind(v("diag", 0, 16), v("stu")), v("iota", 0, C), Alu.mult)
+        total(v("osum"), v("oh"))
+        ts(v("ogu"), last("osum"), 0.0, Alu.add)
+        tt(v("cm2"), v("cmpm"), v("hd1"), Alu.add)
+        act(v("wdec", 0, C), ind(v("cm2"), v("ogu")))
+        act(v("srcw", 0, C), ind(v("nodnr"), v("ogu")))
+        act(v("won"), ind(v("jt16"), v("ogu")))
+        act(v("ownm"), last("wc1"), LT6)
+        tt(v("owng"), v("ownm"), v("cg0"), Alu.add)
+        tt(v("ownsl", 0, K), v("ownm"), v("cs", 0, K), Alu.add)
+        tt(v("ownsl", K, 2 * K), v("ownm"), v("k16") if final else v("cs", K, 2 * K), Alu.add)
+        for b in range(4):
+            mm(4 + b, "qe", "se", b, lf, ls)
+            act(v("wt", 2 * C * b + C, 2 * C * (b + 1)), bank(4 + b), 0.5)
+        tt(first("spc"), v(w1l), v("ownm"), Alu.add)
+        tt(v("cg"), v(w1l), v("owng"), Alu.add)
+        total(v("nbc"), v("spc"))
+        cp(v("cgu"), v("cg"))
+        tt(v("eq"), ind(v("jw"), v("cgu")), v("nbc"), Alu.is_equal)
+        scan(v("seen"), v("keepl"), v("eq"), Alu.mult, Alu.max)
+        tt(v("t12"), last("seen"), v("cg"), Alu.add)
+        ts(v("of2"), v("t12"), 896.0, Alu.min)
+        gather("ab", 1, v("wdec"), "of2")
+        total(v("asum"), v("ab", 1, C + 1))
+        tt(first("ab"), v("stc"), last("asum"), Alu.subtract)
+        scan(v("yq"), v("zero"), v("ab", 0, C), Alu.max, Alu.add)
+        ts(v("hh"), v("yq"), -0.5, Alu.is_equal)
+        tt(v("osl"), v(w2l), v("ownsl"), Alu.add)
+        cp(v("oslu"), v("osl"))
+        tt(v("src1"), ind(v("srcw"), v("oslu", 0, K)), v("hh"), Alu.mult)
+        total(v("src2"), v("src1"))
+        ts(v("srcu"), last("src2"), 0.0, Alu.add)
+        tt(v("lk"), ind(v("won"), v("oslu", K, 2 * K)), v("hh"), Alu.mult)
+        total(v("lsc"), v("lk"))
+        glob("g1", "t13", last("lsc"))
+        if final:
+            act(v("opn"), ind(jt, v("g1")))
+            store("Y", T.op[:], T.opn[0:128:16, :], v("opn")[1])
+        for b in range(4):
+            act(v("hn", C * b, C * (b + 1)), ind(v("wt", 2 * C * b, 2 * C * (b + 1)), v("srcu")))
+        for lo, hi, at in ([(0, H, 0), (H, C, 4)] if final else [(0, C, 0)]):
+            n = hi - lo
+            for b in range(4):
+                z = v("zt", 4 * lo + b, 4 * hi, 4)
+                tt(z, ind(v("hn", C * b, C * (b + 1)), v("invu", lo // 16, hi // 16)),
+                   v("wt", 2 * C * b + lo, 2 * C * b + hi), Alu.add)
+                act(v("z32", C * b + lo, C * b + hi), z, 32.0)
+            quant(v("qz", lo, hi), v("sz", lo, hi), v("zt", 4 * lo, 4 * hi))
+            for b in range(4):
+                x32 = v("x32", C * b + lo, C * b + hi)
+                mm(at + b, "qw", "sw", b, "qz", "sz", lo, n)
+                tt(x32, bank(at + b, n), v("z32", C * b + lo, C * b + hi), Alu.add)
+                if b < 3:
+                    act(v("xt", 4 * lo + b, 4 * hi, 4), x32, 0.03125)
+                else:
+                    ts(v("xt", 4 * lo + b, 4 * hi, 4), x32, 0.03125, Alu.mult)
+            quant(v("qx", lo, hi), v("sx", lo, hi), v("xt", 4 * lo, 4 * hi))
+
+    for lo, at, q in ((0, 0, "S"), (H, 4, "Y")):
+        mm(at, "qv", "sv", 0, "qx", "sx", lo, H)
+        (cp if lo else act)(v("yt", lo, lo + H), bank(at, H))
+        store(q, T.y[:, lo:lo + H], T.yt[:, lo:lo + H], v("yt", lo, lo + H)[1])
+        store("Y", T.oc[:, 4 * lo:4 * (lo + H)], T.qx[:, lo:lo + H].bitcast(dt.uint8), v("qx", lo, lo + H)[1])
+    for k in range(4):
+        store("SY"[k % 2], T.osc[4 * k:4 * k + 4, :], T.sx[32 * k:32 * k + 4, :], v("sx")[1])
+
+    if "line" not in ORDER:
+        ORDER["line"] = _order(ops, list(eng))
+    count = {s: 0 for s in SEMAPHORES}
+    known = {q: {} for q in eng}
+    token = {}
+
+    def wait(q, marks, knew):
+        k = known[q]
+        for s, c in marks:
+            if k.get(s, 0) < c:
+                eng[q].wait_ge(T.sem[s], c)
+                for s2, c2 in list(knew.items()) + [(s, c)]:
+                    if k.get(s2, 0) < c2:
+                        k[s2] = c2
+
+    for i in ORDER["line"]:
+        o = ops[i]
+        q = o["q"]
+        for j in sorted(o["need"], key=lambda j: -token[j][2]):
+            if not (q == "P" and ops[j]["q"] == "P"):
+                wait(q, token[j][0], token[j][1])
+        ins = o["issue"]()
+        if isinstance(o["sem"], tuple):
+            for s in o["sem"]:
+                count[s] += o["inc"]
+            token[i] = ([(s, count[s]) for s in o["sem"]], {}, len(token))
+        else:
+            count[o["sem"]] += o["inc"]
+            ins.then_inc(T.sem[o["sem"]], o["inc"])
+            token[i] = ([(o["sem"], count[o["sem"]])], dict(known[q]), len(token))
+    count["sent"] = sent[0]
+    for s in SEMAPHORES:
+        if count[s]:
+            wait("G", [(s, count[s])], {})

@@ -27,44 +27,52 @@ def _pool(pool, kind, *parts):
     SCRATCH[pool] = ("sbuf", [128, at], kind)
 
 
-_buf("x0 xt ft zt z32 x32 hn", 4 * C, BF)
-_buf("wt", 8 * C, BF)
+_buf("x0 xt ft zt z32 x32", 4 * C, BF)
 _buf("ut vt", 512, BF)
 _buf("et", 2048, BF)
 _buf("idn", 128, BF)
-_buf("qx qz qf0 qf1 qf2 lf0 lf1 lf2", C, F8)
-_buf("sx sz sf0 sf1 sf2 ls0 ls1 ls2", C, U8)
-_buf("qe qw", 512, F8)
-_buf("se sw", 512, U8)
+_buf("qb0 qb1 qb2", 2 * C, F8)
+_buf("sb0 sb1 sb2", 2 * C, U8)
+_buf("qx qz lx0 lx1 lx2 qe0 qe1 qe2 qo0 qo1 qo2", C, F8)
+_buf("sx sz ls0 ls1 ls2 se0 se1 se2 so0 so1 so2", C, U8)
+_buf("qd qde qdo qw", 512, F8)
+_buf("sd sde sdo sw", 512, U8)
 _buf("qu qur qv", 128, F8)
 _buf("su sur sv", 128, U8)
 _buf("nodi pari", K, I32)
 _buf("pidx", 8, I32)
+_buf("half", 8, F32)
 _buf("uli", 8, F32)
 _buf("ulu", 8, U16)
-_buf("nodu np0 np1 np2", K, U16)
+_buf("nodu np0 np1 np2 og0 og1 og2 ol0 ol1 ol2", K, U16)
 _buf("yt opn", C, F32)
-_buf("w1s0 w1s1 w1s2 w1l0 w1l1 w1l2", K, BF)
-_buf("w2s0 w2s1 w2s2 w2l0 w2l1 w2l2", 2 * K, BF)
-_pool("lf32", F32, ("cols ge lt", 16), ("iota srcw", 2 * C), ("cs ownsl osl", 2 * K),
-      ("k16 k256 cg0 stc st16 siz8 vm ownm owng cg key " + " ".join("t%d" % i for i in range(14)), K),
-      ("nodnr sc s1 f1 f2 inv1 inv2 selw", C))
-_pool("lu16", U16, ("c15 d2u invu stu g0 g1 g2 g4 g8 keyu o3u o3q ogu cgu of2 srcu", K), ("oslu", 2 * K))
-_pool("lbf", BF, ("selg jt16 dji diag dpm keep thr keepl selm hd1 zero d2 d4 d8 db c2 c4 c8 pa pb pc pd sel0 siz sell "
-                  "dif cmpm cm2 tmp stn stl xx mx mn spk spc nbk nbc cmk pos g3c g3q wc1 wq eq seen asum won lk lsc "
-                  "yq hh stsc", C),
-      ("jw wdec", 912), ("valt valm tw3 tw2", 256), ("ktab", 544), ("xtab", 16), ("ab", C + 16))
-_pool("lf16", F16, ("h2 h4 h8 oh osum src1 src2", C))
+_buf("ws0 ws1 ws2 wl0 wl1 wl2", K, BF)
+_pool("lf32", F32, ("cols ge gc lt", 16), ("two", 4), ("iota srcw", 2 * C), ("sab far near", 2 * K),
+      ("k16 k256 stc vm ownm owng t0 t1 t2 t3 t8 t9", K),
+      ("nodnr sc s1 f1 f2 inv1 sj sn nw0 nw1 nw2", C))
+_pool("lu16", U16, ("c15 d2u stu g0 g1 g2 g4 keyu o3u cgu of2 sju tu", K), ("pick", 64), ("invu", 2 * K))
+_pool("lbf", BF, ("selg jt16 diag thr d2 d4 d8 db c2 c4 c8 pa pb pc pd siz lsc sel0 "
+                  "dif cmpm stn stl xx spk nbk cmk pos g3c wc1 eq asum won lj rmp rs dtu dng "
+                  "yq hh stsc", C), ("mx sell", 2 * C),
+      ("jt keep ta tb selw", C + 16), ("ab", C + 64), ("wdec", 2 * C + 2), ("valt tw3 tw2 ktab", 256), ("xtab", 16))
+_pool("lf16", F16, ("h2 h4 oh osum spc nbc dse seen trn inv2", C), ("cw dl", 2 * C))
 SCRATCH["ps"] = ("psum", [128, 4096], F32)
 PLACE["ps"] = ("ps", 0, 4096)
 
-LOADS = ["dx", "dnod", "dpar", "du", "dwc", "dws", "dv"]
+LOADS = ["dx", "dnod", "dpar", "du", "dwc", "dws", "dv", "dz"]
 SEMAPHORES = (["qV", "qS", "qP", "qG", "sent", "stored"] + LOADS
-              + ["%s%d" % (n, r) for n in ("an", "af", "as", "aw", "ax") for r in range(3)])
+              + ["%s%d" % (n, r) for n in ("an", "ax", "as", "ao", "av", "aw") for r in range(3)])
 
 Alu = AluOpType
 Act = ActivationFunctionType
-TUNE = dict(word=3.0, big=6.0, wake=0.07, iss=0.02, look=0.3, seed=3, noise=3.0, turns=1200, moves=6)
+PACES = [dict(c=0.00085, t=0.0010, g=0.0012, p=0.0006, call=0.5, same=0.24, wake=0.24, psum=0.0, word=1.3, big=6.0,
+              first=9.0, each=0.0),
+         dict(c=0.00094, t=0.0018, g=0.0010, p=0.0008, call=0.45, same=0.22, wake=0.22, psum=0.0, word=2.1, big=7.0,
+              first=10.0, each=0.0)]
+TUNE = dict(paces=PACES, ex=(0, 4), es=(0, 4), ew=(0, 4), eo=(0, 4), look=0.3, seed=3, turns=10000, slack=0.08, skew=0.0,
+            cut=192, copy="SS", td=(2, 1), whole=0, ft="SSSS", z="SSSVSSSV", z32="SSVVSSVV", xs="SSSSSSSV",
+            g3c="VS", ab="VS", sn="VS", cw="VS", sc="S", t1=2, t2=2, t4=2, t5=1,
+            nbk="V", nbc="V", ws="V", words=1)
 ORDER = {}
 
 
@@ -81,10 +89,18 @@ def _order(ops, queues):
     for i in range(n):
         for j in before[i]:
             after[j].append(i)
-    cost = [o["cost"] + TUNE["iss"] for o in ops]
+    plans = []
+    for pace in TUNE["paces"]:
+        late_ = [pace.get(o["late"], o["late"]) for o in ops]
+        plans.append(([pace["each"] + o["cost"][1] + pace[o["cost"][0]] * o["cost"][2] for o in ops], late_,
+                      [[(j, 0.0 if ops[i]["q"] == ops[j]["q"] == "P" else
+                         late_[j] + pace["same" if ops[i]["q"] == ops[j]["q"] else "wake"]) for j in before[i]]
+                       for i in range(n)]))
+    cost, late, links = plans[0]
+    delay = {(j, i): d for i in range(n) for j, d in links[i]}
 
     def lag(i, j):
-        return 0.0 if ops[i]["q"] == ops[j]["q"] == "P" else ops[i]["late"] + TUNE["wake"]
+        return delay[i, j]
 
     def lay(rank_):
         left = [len(p) for p in before]
@@ -117,27 +133,77 @@ def _order(ops, queues):
 
     way = [0.0] * n
     for i in range(n - 1, -1, -1):
-        way[i] = cost[i] + max([way[j] + lag(i, j) for j in after[i]] + [ops[i]["late"]])
+        way[i] = cost[i] + max([way[j] + lag(i, j) for j in after[i]] + [late[i]])
     seed = [TUNE["seed"]]
 
-    def draw():
+    def draw(m):
         seed[0] = (seed[0] * 6364136223846793005 + 1442695040888963407) % 2 ** 64
-        return (seed[0] >> 33) / 2.0 ** 31
+        return (seed[0] >> 33) % m
 
-    rank_, best = [-w for w in way], None
+    at = lay([-w - o["ahead"] for w, o in zip(way, ops)])
+    line = sorted(range(n), key=lambda i: (at[i], i))
+    queue = [o["q"] for o in ops]
+
+    def play(line_, a, old):
+        new, total = [], 0.0
+        for (cost_, late_, links_), (end, held) in zip(plans, old):
+            end, held = list(end), list(held)
+            prev = {}
+            for i in line_[a - 1::-1] if a else ():
+                if queue[i] not in prev:
+                    prev[queue[i]] = i
+                    if len(prev) == len(queues):
+                        break
+            for i in line_[a:]:
+                h = prev.get(queue[i], -1)
+                t = end[h] if h >= 0 else 0.0
+                for j, d in links_[i]:
+                    if end[j] + d > t:
+                        t, h = end[j] + d, j
+                end[i], held[i] = t + cost_[i], h
+                prev[queue[i]] = i
+            total += max(e + d for e, d in zip(end, late_))
+            new.append((end, held))
+        return total, new
+
+    def waits(state):
+        found = []
+        for (cost_, late_, _), (end, held) in zip(plans, state):
+            i = max(range(n), key=lambda k: end[k] + late_[k])
+            while held[i] >= 0:
+                if held[i] not in ops[i]["need"]:
+                    found.append((held[i], i))
+                i = held[i]
+        return found
+
+    best, state = play(line, 0, [([0.0] * n, [-1] * n) for _ in plans])
+    found, now, keep = waits(state), best, line
     for turn in range(TUNE["turns"]):
-        new = list(rank_)
-        if turn:
-            for _ in range(TUNE["moves"]):
-                i, d = int(draw() * n), TUNE["noise"] * (draw() - 0.5)
-                for j in [i] + (before[i] if d < 0 else after[i]):
-                    new[j] += d
-        at = lay(new)
-        end = max(at[i] + cost[i] + ops[i]["late"] for i in range(n))
-        if best is None or end <= best[0]:
-            best, rank_ = (end, at), new
-    ORDER["end"] = best[0]
-    return sorted(range(n), key=lambda i: (best[1][i], i))
+        p, i = found[draw(len(found))]
+        a, b = line.index(p), line.index(i)
+        early = draw(2)
+        for _ in range(draw(3)):
+            if early:
+                a = next((k for k in range(a - 1, -1, -1) if queue[line[k]] == queue[i]), a)
+            else:
+                b = next((k for k in range(b + 1, n) if queue[line[k]] == queue[i]), b)
+        span = line[a:b + 1]
+        moved = {span[-1] if early else span[0]}
+        for k in (span[-2::-1] if early else span[1:]):
+            if any(j in moved for j in (after[k] if early else before[k])):
+                moved.add(k)
+        if len(moved) == len(span) or (span[0] if early else span[-1]) in moved:
+            continue
+        go, stay = [k for k in span if k in moved], [k for k in span if k not in moved]
+        new = line[:a] + (go + stay if early else stay + go) + line[b + 1:]
+        total, tried = play(new, a, state)
+        if total <= now + TUNE["slack"] * (1 - turn / TUNE["turns"]) * draw(100) / 100:
+            line, now, state = new, total, tried
+            found = waits(state)
+            if now < best:
+                best, keep = now, line
+    ORDER["end"] = best / len(plans)
+    return keep
 
 
 def rank_program(g, core, T, topo):
@@ -147,6 +213,7 @@ def rank_program(g, core, T, topo):
     eng = {"V": g.vector, "S": g.scalar, "P": g.tensor, "G": g, "Y": g.sync}
     ops = []
     acc = {}
+    ahead = [0.0]
 
     def v(name, a=0, b=None, s=1):
         buf, at, n = PLACE[name]
@@ -155,11 +222,29 @@ def rank_program(g, core, T, topo):
         run_ = (a // 512 * 512, (b + 511) // 512 * 512, 1) if buf == "ps" else (a, b, s)
         return (ap, [(buf, run_)], len(range(a, b, s)), SIZE[SCRATCH[buf][2]], False)
 
-    def last(name):
-        return v(name, 15, C, 16)
+    def w(name):
+        return v(name, 0, C)
 
-    def first(name):
-        return v(name, 0, C, 16)
+    def runs(n):
+        return [(K * i // n, K * (i + 1) // n) for i in range(n)]
+
+    def wd(name, p, a=0):
+        return v(name, a + 16 * p[0], a + 16 * p[1])
+
+    def sh(name, p):
+        return v(name, p[0], p[1])
+
+    def upto(name, p):
+        return v(name, 0, 16 * p[1])
+
+    def nth(name, j, p=(0, K)):
+        return v(name, j + 16 * p[0], j + 16 * p[1] - 15, 16)
+
+    def last(name, p=(0, K)):
+        return nth(name, 15, p)
+
+    def first(name, p=(0, K)):
+        return nth(name, 0, p)
 
     def col(j, name="cols"):
         return v(name, j, j + 1)
@@ -172,13 +257,13 @@ def rank_program(g, core, T, topo):
 
     def add(q, issue, reads, writes, cost, late=0.0, sem=None, inc=1):
         need = set()
-        for w, rs in ((False, reads), (True, writes)):
+        for wr, rs in ((False, reads), (True, writes)):
             for name, run_ in rs:
                 for a in acc.get(name, []):
-                    if (w or a[1] or (name == "ps" and a[2] != q)) and _meet(run_, a[0]):
+                    if (wr or a[1] or (name == "ps" and a[2] != q)) and _meet(run_, a[0]):
                         need.add(a[3])
         me = len(ops)
-        ops.append(dict(q=q, issue=issue, need=need, cost=cost, late=late, sem=sem or "q" + q, inc=inc))
+        ops.append(dict(q=q, issue=issue, need=need, cost=cost, late=late, sem=sem or "q" + q, inc=inc, ahead=ahead[0]))
         for name, r_ in writes:
             acc[name] = [a for a in acc.get(name, []) if not (
                 r_[0] <= a[0][0] and a[0][1] <= r_[1] and (r_[2] == 1 or (r_[2] == a[0][2] and _meet(r_, a[0]))))]
@@ -186,22 +271,23 @@ def rank_program(g, core, T, topo):
         for name, r_ in reads:
             acc.setdefault(name, []).append((r_, False, q, me))
 
-    def run(q, fn, out, args, cost, kw=None, more=(), reads=()):
+    def run(q, fn, out, args, cost, kw=None, more=(), reads=(), late=0.0):
         kw = kw or {}
         rd = [r for a in list(args) + list(kw.values()) + list(reads) if isinstance(a, tuple) for r in a[1]]
         wr = list(out[1]) + [r for a in more for r in a[1]]
         pick = lambda a: a[0] if isinstance(a, tuple) else a
         add(q, lambda: fn(out[0], *[a[0] for a in more], *[pick(a) for a in args], **{k: pick(a) for k, a in kw.items()}),
-            rd, wr, cost)
+            rd, wr, cost, late)
 
     def plain(a, per):
-        return 0.055 + a[2] * 0.0013 if a[4] else max(64, a[2] * per) * 0.001
+        return ("g", 0.055, a[2]) if a[4] else ("c", 0.0, max(64, a[2] * per))
 
     def half(*xs):
         return 0.5 if all(x[3] == 2 for x in xs) else 1
 
     def tt(out, a, b, op):
-        run("V", g.vector.tensor_tensor, out, [a, b, op], plain(a, 1 if a[1][0][0] == "ps" else 2 * half(out, a, b)))
+        run("V", g.vector.tensor_tensor, out, [a, b, op],
+            plain(a, 1) if a[4] or a[1][0][0] == "ps" or a[2] <= 32 else ("t", 0.0, a[2]))
 
     def ts(out, a, s1, op0, s2=None, op1=None):
         run("V", g.vector.tensor_scalar, out, [a, s1, s2, op0] + ([] if op1 is None else [op1]), plain(a, half(out, a)))
@@ -209,17 +295,20 @@ def rank_program(g, core, T, topo):
     def cp(out, a):
         run("V", g.vector.tensor_copy, out, [a], plain(a, half(out, a)))
 
+    def turn(out, a):
+        run("V", g.vector.transpose, out, [a], plain(a, half(out, a)))
+
     def scan(out, d0, d1, op0, op1):
         run("V", g.vector.tensor_tensor_scan, out, [d0, d1, 0.0, op0, op1], plain(out, half(out, d0, d1)))
 
     def total(out, d):
-        scan(out, v("keep"), d, Alu.mult, Alu.add)
+        scan(out, v("keep", 0, d[2]), d, Alu.mult, Alu.add)
 
     def fill(out, c):
         run("V", g.vector.memset, out, [c], plain(out, half(out)))
 
     def quant(q, s, a):
-        run("V", g.vector.quantize_mx, q, [a], 0.015 + 0.00028 * a[2], more=[s])
+        run("V", g.vector.quantize_mx, q, [a], ("c", 0.012 + 0.00022 * a[2], 0), more=[s])
 
     def act(out, a, scale=1.0, bias=None, func=None):
         kw = {} if scale == 1.0 else {"scale": scale}
@@ -229,140 +318,153 @@ def rank_program(g, core, T, topo):
             func = Act.Copy if bias is None and not isinstance(scale, tuple) else Act.Identity
         run("S", g.scalar.activation, out, [a, func], plain(a, 1), kw)
 
-    def gather(out, a, win, off):
-        act(v(out, a + H, a + C), ind(win, v(off, K // 2, K)))
-        cp(v(out, a, a + H), ind(win, v(off, 0, K // 2)))
+    def times(q, out, a, c=1.0):
+        if q == "S":
+            act(out, a, c)
+        elif q == "G":
+            run("G", g.affine_select, out, [a, [[0, a[2]]], Alu.is_gt, 0.0, 1, 0], ("c", 0.2, 2 * a[2]))
+        elif c == 1.0:
+            cp(out, a)
+        else:
+            ts(out, a, c, Alu.mult)
+
+    def gather(q, out, a, win, off, p):
+        for h, e_ in zip(runs(2), q) if p == (0, K) and q[0] != q[1] else [(p, q[p[0] // (p[1] - p[0]) % len(q)])]:
+            times(e_, wd(out, h, a), ind(win, sh(off, h)))
+
+    def spread(q, out, hold, short, p, a, b, op):
+        x = first(hold, p) if q == "V" else sh(short, p)
+        tt(x, a, b, op)
+        if q == "V":
+            total(wd(out, p), wd(hold, p))
+        else:
+            act(wd(out, p), ind(v(short, 0, p[1]), sh("kk", p)))
+        return x
 
     def bank(b, n=C):
         return v("ps", 512 * b, 512 * b + n)
 
-    def mm(at, w, ws, b, x, xs, a=0, n=C):
+    def mm(at, wq, ws, b, x, xs, a=0, n=C, start=True, stop=True):
         run("P", g.tensor.matmul_mx, bank(at, n),
-            [v(w, 128 * b, 128 * b + 128), v(ws, 128 * b, 128 * b + 128), v(x, a, a + n), v(xs, a, a + n), True, True],
-            (n + 16) * 0.0006)
+            [v(wq, 128 * b, 128 * b + 128), v(ws, 128 * b, 128 * b + 128), v(x, a, a + n), v(xs, a, a + n), start, stop],
+            ("p", 0.0, n + 16), late="psum")
 
     def iota(out, pattern, base=0, mult=0, small=True):
-        run("G", g.iota, out, [pattern, base, mult], 0.13 + 0.002 * out[2],
+        run("G", g.iota, out, [pattern, base, mult], ("c", 0.15, 2 * out[2]),
             {"allow_small_or_imprecise_dtypes": True} if small else {})
 
-    def load(q, sem, out, src, late):
-        add(q, lambda: eng[q].dma_start(out[0], src), [], out[1], 0.05, late, sem, 16)
+    def load(q, sem, out, src, late, reads=()):
+        add(q, lambda: eng[q].dma_start(out[0], src), reads, out[1], ("c", 0.05, 0), late, sem, 16)
 
     def store(q, dst, ap, reads):
-        add(q, lambda: eng[q].dma_start(dst, ap), reads, [], 0.05, 2.5, "stored", 16)
+        add(q, lambda: eng[q].dma_start(dst, ap), reads, [], ("c", 0.05, 0), 2.2, "stored", 16)
 
     def peer(r):
         return T.cores[rank ^ ROUNDS[r]]
 
     sent = [0]
 
-    def send(dst, land, src, sem, part, late):
-        e = topo.engines(core, dst)
-        n = len(e) // 2
-        m = sum(1 << k for k in e[part * n:(part + 1) * n])
-        rid, pid, _ = topo.addr(dst)
-        sent[0] += n
-        add("G", lambda: g.remote_dma(land[0], src[0], T.sem[sem], T.sem.sent, pid, rid, m), src[1], land[1], 0.3, late,
-            (sem,), n)
+    reach = [k for k in topo.engines(core, peer(0)) if all(k in topo.engines(core, peer(j)) for j in range(3))]
 
-    PM, CA, CB, ST, O3, MQ, ML, I16, MUT, ST4, GL, T0, T1, T2, T3, T4 = range(16)
-    GE6, GE14, E15, LT6, LT15 = col(6, "ge"), col(14, "ge"), col(15, "ge"), col(6, "lt"), col(15, "lt")
+    def send(dst, land, src, sem, late, share):
+        e_ = reach[len(reach) * share[0] // 4:len(reach) * share[1] // 4]
+        rid, pid, _ = topo.addr(dst)
+        sent[0] += len(e_)
+        add("G", lambda: g.remote_dma(land[0], src[0], T.sem[sem], T.sem.sent, pid, rid, sum(1 << k for k in e_)),
+            src[1], land[1], ("call", 0.0, 1), late, (sem,), len(e_))
+
+    PM, CA, CB, ST, I16, GL, E15B = range(7)
+    GE6, E15, LT6, LT14, LT15 = col(6, "ge"), col(15, "ge"), col(6, "lt"), col(14, "lt"), col(15, "lt")
+    parts = [(0, TUNE["cut"], 0), (TUNE["cut"], C, 4)]
 
     load("Y", "dx", v("x0"), T.x[:], 3.2)
-    load("S", "dnod", v("nodi"), T.nod[:], 2.1)
     load("S", "dpar", v("pari"), T.par[:], 2.1)
+    load("S", "dnod", v("nodi"), T.nod[:], 2.1)
     load("S", "du", v("ut"), T.u[:], 2.6)
     load("Y", "dwc", bits(v("qw"), dt.uint8), T.wc[:], 4.0)
     load("Y", "dws", v("sw"), T.ws[:], 4.0)
     load("Y", "dv", v("vt"), T.v[:], 4.0)
 
-    jt = v("jw", 0, C)
+    jt = w("jt")
     iota(v("pidx", 0, 1), [[0, 1]], 0, 1, False)
-    iota(jt, [[0, K], [1, 16]])
+    fill(v("keep"), 1.0)
+    fill(v("keep", 0, C + 16, 16), 0.0)
+    total(v("jt"), v("keep"))
     iota(v("k16"), [[16, K]])
+    iota(v("k256"), [[256, K]])
     iota(v("uli"), [[16, 8]])
-    iota(v("idn"), [[1, 128]], 0, -1)
-    iota(v("iota"), [[1, 2 * C]])
+    iota(v("iota", 0, C), [[1, C]])
     iota(v("valt"), [[1, 16], [0, 16]])
-    iota(v("selg"), [[256, K], [0, 16]], 256)
+    iota(v("idn"), [[1, 128]], 0, -1)
+    iota(v("ktab"), [[16, 256]])
+    iota(v("xtab"), [[256, 16]])
+    for name, c in (("spk", 0), ("rmp", -1), ("dtu", 1), ("dng", 1)):
+        iota(v(name), [[0, C]], c)
+    iota(v("wdec", 0, 2 * C + 2, 2), [[0, C + 1]], -1)
+    act(v("iota", C, 2 * C), v("iota", 0, C), 1.0, float(C))
     ts(v("pidx", 1, 2), v("pidx", 0, 1), 15, Alu.bitwise_and)
+    ts(v("pidx", 2, 3), v("pidx", 0, 1), 16, Alu.bitwise_and)
     cp(col(PM), v("pidx", 1, 2))
-    ts(v("ge"), v("jw", 0, 16), col(PM), Alu.is_le)
-    ts(v("lt"), v("jw", 0, 16), col(PM), Alu.is_gt)
-    ts(v("dji"), jt, col(PM), Alu.subtract)
+    ts(col(0, "half"), v("pidx", 2, 3), 0.0, Alu.is_equal)
+    ts(col(1, "half"), v("pidx", 2, 3), 0.0, Alu.is_gt)
+    ts(v("ge"), v("jt", 0, 16), col(PM), Alu.is_le)
+    ts(v("gc"), v("jt", 0, 16), col(PM), Alu.is_le, float(C), Alu.mult)
+    ts(v("lt"), v("jt", 0, 16), col(PM), Alu.is_gt)
     act(col(I16), col(PM), 16.0)
-    act(col(ST), LT15, 256.0)
-    act(col(ST4), LT15, 1024.0)
-    act(col(O3), LT15, 256.0, 4096.0)
+    act(col(ST), LT15, 1024.0)
+    act(col(CA), LT15, 2.0, col(PM))
     act(col(CB), LT15, 1.0, 14.0)
-    act(col(T0), LT15, 2.0, -1.0)
-    act(col(CA), col(PM), 1.0, col(T0))
-    act(col(MUT), col(I16), 1.0, col(ST))
-    act(col(MQ), GE14, -1.0, GE6)
-    act(col(ML), E15, -1.0, GE6)
-    act(col(T1), col(MQ), 384.0)
-    act(col(T2), E15, 15.0)
-    act(col(T3), E15, 512.0)
-    act(col(GL), col(1, "lt"), 8192.0, -256.0)
-    act(v("cs", 0, K), v("k16"), 1.0, col(T1))
-    act(v("cs", K, 2 * K), v("k16"), 1.0, col(T2))
-    act(v("cg0"), v("k16"), 1.0, col(T3))
+    act(col(E15B), E15, 2000.0)
+    act(col(GL), col(1, "lt"), 8192.0, -1024.0)
     act(v("jt16"), jt, 16.0)
-    act(v("k256"), v("k16"), 16.0)
-    ts(v("diag"), v("dji"), 0.0, Alu.is_equal)
-    ts(v("keep"), jt, 1.0, Alu.min)
-    act(v("dpm"), v("diag", 0, 256) if False else v("diag"), 2.0, -1.0)
-    act(v("hd1"), v("diag"), 0.5, -1.0)
-    act(v("eq"), v("diag"), -1024.0)
-    ts(v("seen"), v("dji"), 1.0, Alu.is_equal, 256.0, Alu.mult)
-    tt(v("selm"), v("eq"), v("seen"), Alu.add)
-    act(v("selw"), v("selm"), 4.0)
-    tt(v("selg"), v("selg"), v("diag"), Alu.mult)
-    ts(v("tmp"), v("dji"), -1.0, Alu.is_equal, -8192.0, Alu.mult)
-    ts(last("tmp"), last("dji"), 15.0, Alu.is_equal, -8192.0, Alu.mult)
-    tt(v("selg"), v("selg"), v("tmp"), Alu.add)
+    ts(w("diag"), jt, col(PM), Alu.is_equal)
+    ts(v("ta"), v("jt"), col(PM), Alu.is_equal, -8192.0, Alu.mult)
+    act(v("tb"), v("ta"), 2.0 ** -16)
+    scan(v("selw", 0, C + 1), v("tb", 15, C + 16), v("ta", 0, C + 1), Alu.mult, Alu.add)
+    act(v("selg"), v("selw", 1, C + 1))
+    tt(last("selg"), last("selg"), v("k256"), Alu.add)
     ts(v("c15"), v("k16"), 15.0, Alu.add)
-    ts(v("thr"), v("dji"), 0.0, Alu.is_lt, 2.0 ** -110, Alu.mult)
-    act(v("xtab"), v("iota", 0, 16), 256.0, 256.0)
-    act(v("ktab"), v("iota", 0, 544), 16.0, -4224.0, Act.Abs)
-    ts(v("tw3"), v("jw", 0, 256), col(CA), Alu.is_equal)
-    ts(v("valm"), v("valt"), col(CB), Alu.min)
-    tt(v("tw3"), v("tw3"), v("valm"), Alu.mult)
-    ts(v("tw2"), v("valt"), col(PM), Alu.is_equal, 2.0, Alu.mult)
-    ts(v("tw2"), v("tw2"), -1.0, Alu.add)
-    tt(v("tw2"), v("tw2"), v("dpm", 0, 256), Alu.max)
-    act(v("spk"), jt, 0.0)
-    act(v("spc"), jt, 0.0)
-    act(v("zero"), jt, 0.0)
-    act(v("jw", C), v("iota", 0, 912 - C), 0.0, 31.0)
-    act(v("wdec", C), v("iota", 0, 912 - C), 0.0, -1.0)
-    ts(v("keepl"), v("dji"), 1.0, Alu.not_equal)
-    act(last("keepl"), last("keepl"), 512.0)
-    act(first("keepl"), first("keepl"), 0.0)
-    fill(v("et"), 0.0)
-    for b in range(4):
-        ts(v("et", 512 * b + b, 512 * (b + 1), 4), v("idn"), 0.0, Alu.is_equal)
-    quant(v("qe"), v("se"), v("et"))
+    ts(v("thr"), jt, col(PM), Alu.is_lt, 2.0 ** -110, Alu.mult)
+    ts(v("tw3"), v("jt", 0, 256), 1.0, Alu.add, col(CA), Alu.is_equal)
+    tt(v("tw3"), v("tw3"), v("valt"), Alu.mult)
+    ts(v("tw2"), v("valt"), col(PM), Alu.is_equal)
+    tt(v("tw2"), v("tw2"), v("diag", 0, 256), Alu.max)
+    ts(v("spc"), jt, 0.0, Alu.mult)
+    act(last("dtu"), v("k16"), -1.0, -128.0)
+    act(last("dng"), v("k16"), 0.0, -1.0)
+    act(v("dse"), w("diag"), -1024.0)
+    act(last("dse"), v("k16"), 0.0, -1024.0)
+    ts(v("idn"), v("idn"), 0.0, Alu.is_equal)
+    fill(v("et", 0, 1024), 0.0)
+    load("Y", "dz", v("et", 1024, 2048), T.et[:, 0:1024], 2.3, v("et", 0, 1024)[1])
+    for q, s, m in (("qd", "sd", 1.0), ("qde", "sde", col(0, "half")), ("qdo", "sdo", col(1, "half"))):
+        for b in range(4):
+            act(v("et", 512 * b + b, 512 * (b + 1), 4), v("idn"), m)
+        quant(v(q), v(s), v("et"))
     cp(v("ulu"), v("uli"))
     quant(v("qu"), v("su"), v("ut"))
     cp(bits(v("qur"), dt.uint32), ind(bits(v("qu"), dt.uint32), v("ulu")))
     act(v("sur"), ind(v("su"), v("ulu")))
     quant(v("qv"), v("sv"), v("vt"))
 
-    def glob(out, tmp, loc):
+    def glob(out, tmp, loc, off=None):
         tt(v(tmp), loc, v("k256"), Alu.add)
-        ts(v(out), v(tmp), 0.0625, Alu.mult)
+        if off is None:
+            ts(v(out), v(tmp), 0.0625, Alu.mult)
+        else:
+            ts(v(out), v(tmp), off, Alu.subtract, 0.0625, Alu.mult)
 
-    def diagonal(out, x, hold="selm"):
-        scan(out, v(hold), x, Alu.add, Alu.max)
+    def diagonal(out, x):
+        scan(out, v("selw", 0, x[2]), x, Alu.add, Alu.max)
 
-    def places(out, tmp, x):
-        scan(v(tmp), v(x), v("selg"), Alu.max, Alu.add)
-        ts(v(out), last(tmp), col(GL), Alu.add, 0.0625, Alu.mult)
+    def places(out, tmp, x, p):
+        scan(wd(tmp, p), wd(x, p), wd("selg", p), Alu.max, Alu.add)
+        ts(sh(out, p), last(tmp, p), col(GL), Alu.add, 0.0625, Alu.mult)
 
+    ahead[0] = 30.0
     cp(v("nodu"), v("nodi"))
     moves = []
-    e = [k for k in topo.engines(core, peer(0)) if all(k in topo.engines(core, peer(j)) for j in range(3))]
+    e = reach
     n = len(e) // 4
     for r in range(3):
         rid, pid, _ = topo.addr(peer(r))
@@ -371,166 +473,178 @@ def rank_program(g, core, T, topo):
                                        src=T.nodu[:], dst=T["np%d" % r][:]))
     sent[0] += 3 * n
     add("G", lambda: g.remote_dma_fused(moves, local_sem=T.sem.sent), v("nodu")[1],
-        v("np0")[1] + v("np1")[1] + v("np2")[1], 2.0, 4.0, ("an0", "an1", "an2"), n)
+        v("np0")[1] + v("np1")[1] + v("np2")[1], ("call", 0.0, 1), "first", ("an0", "an1", "an2"), n)
+    ahead[0] = 0.0
     act(v("nodnr"), ind(v("iota", 0, C), v("nodu")))
-    run("V", g.vector.tensor_copy, (ind(v("inv1"), v("nodu"))[0], v("inv1")[1]), [v("iota", 0, C)], 1.3, reads=[v("nodu")])
-    diagonal(v("inv2"), v("inv1"), "selw")
-    ts(v("invu"), last("inv2"), col(ST4), Alu.subtract)
+    run("V", g.vector.tensor_copy, (ind(v("inv1"), v("nodu"))[0], v("inv1")[1]), [v("iota", 0, C)], ("g", 0.05, 2 * C),
+        reads=[v("nodu")])
+    diagonal(v("inv2"), v("inv1"))
+    for o in (0, 1):
+        ts(v("invu", o, 2 * K, 2), last("inv2"), col(ST), Alu.subtract)
 
-    ts(last("lsc"), v("pari"), 16.0, Alu.mult)
-    glob("g0", "t0", last("lsc"))
-    act(v("pc"), ind(v("jt16"), v("g0")))
-    act(v("pd"), ind(v("pc"), v("g0")))
-    ts(v("t1"), last("lsc"), col(I16), Alu.is_gt)
-    ts(v("t2"), last("lsc"), -1.0, Alu.mult, col(I16), Alu.add)
-    tt(v("t1"), v("t1"), v("t2"), Alu.mult)
-    diagonal(v("sel0"), v("pd"))
-    ts(v("t3"), last("sel0"), col(MUT), Alu.is_equal)
-    tt(v("t1"), v("t1"), v("t3"), Alu.mult)
-    tt(last("lsc"), last("lsc"), v("t1"), Alu.add)
-    glob("g1", "t0", last("lsc"))
-    quant(v("qx"), v("sx"), v("x0"))
+    ts(v("g0"), v("pari"), 16.0, Alu.mult, col(PM), Alu.add)
+    ts(first("spk"), v("pari"), col(I16), Alu.add)
+    total(v("nbk"), v("spk"))
+    tt(v("cmk"), ind(v("iota", 0, 256), v("g0")), v("nbk"), Alu.is_equal)
+    total(v("pos"), v("cmk"))
+    ts(v("t1"), v("pari"), col(PM), Alu.subtract, 0.0, Alu.max)
+    cp(v("t2"), v("pari"))
+    tt(v("t0"), v("t2"), v("k16"), Alu.add)
+    tt(v("t1"), v("t1"), last("pos"), Alu.mult)
+    tt(v("t0"), v("t0"), v("t1"), Alu.subtract)
+    tt(v("t2"), v("t2"), v("t1"), Alu.subtract)
+    cp(v("g1"), v("t0"))
+    ts(v("d2u"), v("t2"), 16.0, Alu.mult, col(PM), Alu.add)
+    act(v("pa"), ind(v("jt16"), v("g1")))
+    quant(v("qb0", 0, C), v("sb0", 0, C), v("x0"))
 
     for r in range(3):
         to = peer(r)
         final = r == 2
-        qf, sf, lf, ls = ("qf%d" % r, "sf%d" % r, "lf%d" % r, "ls%d" % r)
-        w1s, w1l, w2s, w2l = ("w1s%d" % r, "w1l%d" % r, "w2s%d" % r, "w2l%d" % r)
-        act(v("pa"), ind(v("jt16"), v("g1")))
-        act(v("pb"), ind(v("pa"), v("g1")))
-        ts(v("d2u"), last("lsc"), col(PM), Alu.add)
-        act(v("d2"), ind(v("tw2"), v("d2u")))
-        cp(v("c2"), v("d2"))
-        places("g2", "h2", "pb")
-        act(v("pc"), ind(v("pb"), v("g2")))
-        tt(v("d4"), ind(v("d2"), v("g2")), v("c2"), Alu.max)
-        act(v("c4"), v("d4"))
-        places("g4", "h4", "pc")
-        act(v("pd"), ind(v("pc"), v("g4")))
-        tt(v("d8"), ind(v("d4"), v("g4")), v("c4"), Alu.max)
-        act(v("c8"), v("d8"))
-        places("g8", "h8", "pd")
-        tt(v("db"), ind(v("d8"), v("g8")), v("c8"), Alu.max)
-        total(v("siz"), v("db"))
-        act(v("siz8"), last("siz"), 8.0)
-        mm(4, "qur", "sur", 0, "qx", "sx")
-        act(v("sc"), bank(4))
-        for b in range(4):
-            mm(b, "qe", "se", b, "qx", "sx")
-        act(v("s1"), ind(v("sc"), v("nodu")))
-        tt(v("f1"), ind(v("sc"), v("nodu")), v("diag"), Alu.mult)
-        total(v("f2"), v("f1"))
-        tt(v("dif"), ind(v("f2"), v("c15")), v("s1"), Alu.subtract)
-        tt(v("cmpm"), v("dif"), v("thr"), Alu.is_lt)
-        total(v("stsc"), v("cmpm"))
-        ts(v("stu"), last("stsc"), 0.0, Alu.add)
-        act(v("stn"), ind(v("jt16", 0, 16), v("stu")))
-        act(v("stl"), ind(v("stn"), v("g1")))
-        act(v("st16"), last("stsc"), 16.0, col(ST))
+        qb, sb, lx, ls, qe, se, qo, so, og, ol, ws, wl, nw = (
+            n + str(r) for n in ("qb", "sb", "lx", "ls", "qe", "se", "qo", "so", "og", "ol", "ws", "wl", "nw"))
+        send(to, bits(v(lx), dt.uint8), bits(v(qb, 0, C), dt.uint8), "ax%d" % r, "big" if r else "first", TUNE["ex"])
+        send(to, v(ls), v(sb, 0, C), "as%d" % r, "big" if r else "first", TUNE["es"])
+        for p in runs(TUNE["td"][r > 0]):
+            act(wd("pb", p), ind(upto("pa", p), sh("g1", p)))
+            act(wd("d2", p), ind(v("tw2"), sh("d2u", p)), 2.0, -1.0)
+            times(TUNE["copy"][0], wd("c2", p), wd("d2", p))
+            places("g2", "h2", "pb", p)
+            act(wd("pc", p), ind(upto("pb", p), sh("g2", p)))
+            tt(wd("d4", p), ind(upto("d2", p), sh("g2", p)), wd("c2", p), Alu.max)
+            times(TUNE["copy"][1], wd("c4", p), wd("d4", p))
+            places("g4", "h4", "pc", p)
+            tt(wd("d8", p), ind(upto("d4", p), sh("g4", p)), wd("c4", p), Alu.max)
+            act(wd("c8", p), ind(upto("d8", p), sh("g4", p)))
+            tt(wd("db", p), ind(upto("c8", p), sh("g4", p)), wd("d8", p), Alu.max)
+            total(wd("siz", p), wd("db", p))
+        for i, (lo, hi, _) in enumerate(parts if r else [(0, C, 0)]):
+            mm(i, "qur", "sur", 0, qb, sb, lo, hi - lo)
+            times(TUNE["sc"], v("sc", lo, hi), bank(i, hi - lo))
+        for p in runs(TUNE["t1"]):
+            act(wd("s1", p), ind(v("sc"), sh("nodu", p)))
+            tt(wd("f1", p), ind(v("sc"), sh("nodu", p)), wd("diag", p), Alu.mult)
+            total(wd("f2", p), wd("f1", p))
+            tt(wd("dif", p), ind(upto("f2", p), sh("c15", p)), wd("s1", p), Alu.subtract)
+            tt(wd("cmpm", p), wd("dif", p), wd("thr", p), Alu.is_lt)
+            total(wd("stsc", p), wd("cmpm", p))
+            ts(sh("stu", p), last("stsc", p), 0.0, Alu.add)
         act(v("stc"), last("stsc"), 1.0, -16.5)
-        for b in range(4):
-            act(v("ft", b, 4 * C, 4), bank(b))
-        quant(v(qf), v(sf), v("ft"))
-        send(to, bits(v(lf), dt.uint8), bits(v(qf), dt.uint8), "af%d" % r, 0, TUNE["big"])
-        send(to, v(ls), v(sf), "as%d" % r, 0, TUNE["big"])
-        for b in range(4):
-            act(v("wt", 2 * C * b, 2 * C * b + C), bank(b), 0.5)
-        act(v("srcw", C, 2 * C), ind(v("iota", C, 2 * C), v("np%d" % r)))
-        tt(v("xx"), ind(v("xtab"), v("stu")), v("db"), Alu.mult)
-        scan(v("mx"), v("keep"), v("xx"), Alu.mult, Alu.max)
-        scan(v("mn"), v("keep"), v("xx"), Alu.mult, Alu.min)
-        tt(v("t4"), last("mx"), v("siz8"), Alu.add)
-        tt(v("key"), v("t4"), last("mn"), Alu.add)
-        act(first("spk"), v("key"), func=Act.Abs)
-        ts(v("keyu"), v("key"), 0.0625, Alu.mult, 264.0, Alu.add)
-        total(v("nbk"), v("spk"))
-        tt(v("cmk"), ind(v("ktab"), v("keyu")), v("nbk"), Alu.is_gt)
-        total(v("pos"), v("cmk"))
-        diagonal(v("sell"), v("stl"))
-        tt(v("t5"), last("mx"), v("st16"), Alu.add)
-        tt(v("t6"), last("sell"), last("mn"), Alu.subtract)
-        tt(v("vm"), v("t5"), v("t6"), Alu.max)
-        tt(v("t7"), v("vm"), last("pos"), Alu.add)
-        ts(v("o3u"), v("t7"), col(O3), Alu.subtract)
-        gather("g3c", 0, v("tw3"), "o3u")
-        total(v("wc1"), v("g3c"))
-        ts(v(w1s), last("wc1"), GE6, Alu.mult)
-        send(to, v(w1l), v(w1s), "aw%d" % r, 1, TUNE["word"])
-        act(v("t8"), last("mx"), 1.0, col(I16))
-        tt(v("t9"), last("lsc"), last("mn"), Alu.subtract)
-        tt(v("t9"), v("t8"), v("t9"), Alu.max)
-        tt(v("t9"), v("t9"), last("pos"), Alu.add)
-        ts(v("o3q"), v("t9"), 4096.0, Alu.subtract)
-        act(v("g3q"), ind(v("tw3"), v("o3q")))
-        total(v("wq"), v("g3q"))
-        act(v("t10"), last("wc1"), GE14)
-        act(v("t11"), last("wq"), col(MQ))
-        act(v(w2s, K, 2 * K), last("wc1"), GE6 if final else col(ML))
-        tt(v(w2s, 0, K), v("t10"), v("t11"), Alu.add)
-        send(to, v(w2l), v(w2s), "ax%d" % r, 1, TUNE["word"])
+        act(first("rmp"), last("stsc"), 1.0, -0.5)
+        for p in runs(TUNE["t2"]):
+            ahead[0] = 0.0 if p[0] else TUNE["skew"]
+            both = (2 * p[0], 2 * p[1])
+            low, high = (2 * p[0], p[0] + p[1]), (p[0] + p[1], 2 * p[1])
+            act(sh("sab", low), last("siz", p), 8.0, 128.0)
+            act(sh("sab", high), last("siz", p), -8.0, 128.0)
+            act(last("sell", low), last("stsc", p), 16.0, col(ST))
+            act(wd("stn", p), ind(v("jt16", 0, 16), sh("stu", p)))
+            act(wd("stl", p), ind(upto("stn", p), sh("g1", p)))
+            tt(wd("xx", p), ind(v("xtab"), sh("stu", p)), wd("db", p), Alu.mult)
+            scan(wd("mx", low), wd("keep", p), wd("xx", p), Alu.mult, Alu.max)
+            scan(wd("mx", high), wd("xx", p), wd("dng", p), Alu.min, Alu.mult)
+            tt(sh("far", both), last("mx", both), sh("sab", both), Alu.add)
+            tt(first("spk", p), sh("far", low), sh("far", high), Alu.min)
+            total(wd("nbk", p), wd("spk", p))
+            ts(sh("keyu", p), first("spk", p), 0.0625, Alu.mult)
+            tt(wd("cmk", p), ind(v("ktab"), sh("keyu", p)), wd("nbk", p), Alu.is_lt)
+            total(wd("pos", p), wd("cmk", p))
+            diagonal(wd("sell", high), wd("stl", p))
+            tt(sh("near", both), last("mx", both), last("sell", both), Alu.add)
+            tt(sh("vm", p), sh("near", low), sh("near", high), Alu.max)
+            tt(sh("t8", p), sh("vm", p), last("pos", p), Alu.add)
+            ts(sh("o3u", p), sh("t8", p), col(ST), Alu.subtract, 3840.0, Alu.subtract)
+            gather(TUNE["g3c"], "g3c", 0, v("tw3"), "o3u", p)
+            total(wd("wc1", p), wd("g3c", p))
+            ts(sh(ws, p), last("wc1", p), GE6, Alu.mult, col(CB), Alu.min)
+        ahead[0] = 0.0
+        for i, p in enumerate(runs(TUNE["words"])):
+            send(to, sh(wl, p), sh(ws, p), "a%s%d" % ("wv"[i], r), "word", TUNE["ew"])
         tt(v("oh"), ind(v("diag", 0, 16), v("stu")), v("iota", 0, C), Alu.mult)
         total(v("osum"), v("oh"))
-        ts(v("ogu"), last("osum"), 0.0, Alu.add)
-        tt(v("cm2"), v("cmpm"), v("hd1"), Alu.add)
-        act(v("wdec", 0, C), ind(v("cm2"), v("ogu")))
-        act(v("srcw", 0, C), ind(v("nodnr"), v("ogu")))
-        act(v("won"), ind(v("jt16"), v("ogu")))
-        act(v("ownm"), last("wc1"), LT6)
-        tt(v("owng"), v("ownm"), v("cg0"), Alu.add)
-        tt(v("ownsl", 0, K), v("ownm"), v("cs", 0, K), Alu.add)
-        tt(v("ownsl", K, 2 * K), v("ownm"), v("k16") if final else v("cs", K, 2 * K), Alu.add)
+        ts(v(og), last("osum"), 0.0, Alu.add)
+        send(to, v(ol), v(og), "ao%d" % r, "word", TUNE["eo"])
+        total(v("rs"), v("rmp"))
+        ts(v("wdec", 1, 2 * C, 2), v("rs"), -1.0, Alu.max, 0.0, Alu.min)
+        act(v("srcw", 0, C), ind(v("nodnr"), v(og)))
+        act(v("won"), ind(v("jt16"), v(og)))
+        act(v(nw), ind(v("iota", C, 2 * C), v("np%d" % r)))
+        act(v("srcw", C, 2 * C), ind(v(nw), v(ol)))
+        for p in runs(TUNE["words"]):
+            act(sh("ownm", p), last("wc1", p), LT6)
+            tt(sh("owng", p), sh("ownm", p), sh("k16", p), Alu.add)
         for b in range(4):
-            mm(4 + b, "qe", "se", b, lf, ls)
-            act(v("wt", 2 * C * b + C, 2 * C * (b + 1)), bank(4 + b), 0.5)
-        tt(first("spc"), v(w1l), v("ownm"), Alu.add)
-        tt(v("cg"), v(w1l), v("owng"), Alu.add)
-        total(v("nbc"), v("spc"))
-        cp(v("cgu"), v("cg"))
-        tt(v("eq"), ind(v("jw"), v("cgu")), v("nbc"), Alu.is_equal)
-        scan(v("seen"), v("keepl"), v("eq"), Alu.mult, Alu.max)
-        tt(v("t12"), last("seen"), v("cg"), Alu.add)
-        ts(v("of2"), v("t12"), 896.0, Alu.min)
-        gather("ab", 1, v("wdec"), "of2")
-        total(v("asum"), v("ab", 1, C + 1))
-        tt(first("ab"), v("stc"), last("asum"), Alu.subtract)
-        scan(v("yq"), v("zero"), v("ab", 0, C), Alu.max, Alu.add)
-        ts(v("hh"), v("yq"), -0.5, Alu.is_equal)
-        tt(v("osl"), v(w2l), v("ownsl"), Alu.add)
-        cp(v("oslu"), v("osl"))
-        tt(v("src1"), ind(v("srcw"), v("oslu", 0, K)), v("hh"), Alu.mult)
-        total(v("src2"), v("src1"))
-        ts(v("srcu"), last("src2"), 0.0, Alu.add)
-        tt(v("lk"), ind(v("won"), v("oslu", K, 2 * K)), v("hh"), Alu.mult)
-        total(v("lsc"), v("lk"))
-        glob("g1", "t13", last("lsc"))
+            mm(4 + b, "qd", "sd", b, lx, ls)
+            times(TUNE["ft"][b], v("ft", b, 4 * C, 4), bank(4 + b))
+        quant(v(qb, C, 2 * C), v(sb, C, 2 * C), v("ft"))
+        for p in runs(TUNE["t4"]):
+            at = 16 * (p[0] // (p[1] - p[0]))
+            cg = first("spc", p)
+            tt(cg, sh(wl, p), sh("owng", p), Alu.add)
+            total(wd("nbc", p), wd("spc", p))
+            ts(sh("cgu", p), cg, 0.0, Alu.add)
+            act(nth("dse", 14, p), cg, 2.0, LT14)
+            ts(sh("sju", p), cg, col(6, "gc"), Alu.add, col(14, "gc"), Alu.subtract)
+            tt(wd("eq", p), ind(v("iota", 0, C), sh("cgu", p)), wd("nbc", p), Alu.is_equal)
+            scan(wd("seen", p), wd("eq", p), wd("dse", p), Alu.max, Alu.add)
+            ts(sh("of2", p), nth("seen", 14, p), col(E15B), Alu.max, 2.0 * C, Alu.min)
+            gather(TUNE["ab"], "ab", at + 1, v("wdec", 0, 2 * C + 1), "of2", p)
+            total(wd("asum", p), wd("ab", p, at + 1))
+            tt(nth("ab", at, p), sh("stc", p), last("asum", p), Alu.subtract)
+            scan(wd("yq", p), wd("thr", p), wd("ab", p, at), Alu.max, Alu.add)
+            ts(wd("hh", p), wd("yq", p), -0.5, Alu.is_equal, 113.0, Alu.mult)
+            scan(wd("trn", p), wd("hh", p), wd("dtu", p), Alu.max, Alu.add)
+            ts(sh("tu", p), last("trn", p), -1.0, Alu.mult)
+            act(wd("sj", p), ind(v("srcw"), sh("sju", p)))
+            gather(TUNE["sn"], "sn", 0, upto("sj", p), "tu", p)
+        act(v("lj"), ind(v("won"), v("cgu")))
+        if not final:
+            act(last("lj"), last("won"))
+        for i, (lo, hi, _) in enumerate(parts):
+            times(TUNE["cw"][i], v("cw", 2 * lo, 2 * hi), ind(v("sn"), v("invu", lo // 8, hi // 8)))
+            turn(v("dl", 2 * lo, 2 * hi), v("cw", 2 * lo, 2 * hi))
+            for o in (0, 1):
+                ts(v("pick", 32 * o + lo // 16, 32 * o + hi // 16), v("dl", 2 * lo + 16 * o, 2 * hi, 32), 0.0, Alu.add)
         if final:
-            act(v("opn"), ind(jt, v("g1")))
+            act(v("opn"), ind(v("lj"), v("tu")), 0.0625)
             store("Y", T.op[:], T.opn[0:128:16, :], v("opn")[1])
-        for b in range(4):
-            act(v("hn", C * b, C * (b + 1)), ind(v("wt", 2 * C * b, 2 * C * (b + 1)), v("srcu")))
-        for lo, hi, at in ([(0, H, 0), (H, C, 4)] if final else [(0, C, 0)]):
+        for p in [] if final else runs(TUNE["td"][1]):
+            act(wd("pa", p), ind(upto("lj", p), sh("tu", p)))
+            diagonal(wd("lsc", p), wd("pa", p))
+            ts(sh("d2u", p), last("lsc", p), col(ST), Alu.subtract, col(PM), Alu.add)
+            tt(sh("t9", p), last("lsc", p), sh("k256", p), Alu.add)
+            ts(sh("g1", p), sh("t9", p), col(ST), Alu.subtract, 0.0625, Alu.mult)
+        nq, ns = ("qx", "sx") if final else ("qb%d" % (r + 1), "sb%d" % (r + 1))
+        for lo, hi, at in parts:
             n = hi - lo
+            for q, s, o in ((qe, se, 0), (qo, so, 32)):
+                off = v("pick", o + lo // 16, o + hi // 16)
+                cp(bits(v(q, lo, hi), dt.uint32), ind(bits(v(qb), dt.uint32), off))
+                act(v(s, lo, hi), ind(v(sb), off))
             for b in range(4):
-                z = v("zt", 4 * lo + b, 4 * hi, 4)
-                tt(z, ind(v("hn", C * b, C * (b + 1)), v("invu", lo // 16, hi // 16)),
-                   v("wt", 2 * C * b + lo, 2 * C * b + hi), Alu.add)
-                act(v("z32", C * b + lo, C * b + hi), z, 32.0)
+                mm(at + b, "qd", "sd", b, qb, sb, lo, n, True, False)
+            for b in range(4):
+                mm(at + b, "qde", "sde", b, qe, se, lo, n, False, False)
+            for b in range(4):
+                mm(at + b, "qdo", "sdo", b, qo, so, lo, n, False, True)
+                times(TUNE["z"][at + b], v("zt", 4 * lo + b, 4 * hi, 4), bank(at + b, n), 0.5)
             quant(v("qz", lo, hi), v("sz", lo, hi), v("zt", 4 * lo, 4 * hi))
+            if TUNE["whole"]:
+                times("V", v("z32", 4 * lo, 4 * hi), v("zt", 4 * lo, 4 * hi), 32.0)
             for b in range(4):
-                x32 = v("x32", C * b + lo, C * b + hi)
+                at4 = (4 * lo + b, 4 * hi, 4)
+                if not TUNE["whole"]:
+                    times(TUNE["z32"][at + b], v("z32", *at4), v("zt", *at4), 32.0)
                 mm(at + b, "qw", "sw", b, "qz", "sz", lo, n)
-                tt(x32, bank(at + b, n), v("z32", C * b + lo, C * b + hi), Alu.add)
-                if b < 3:
-                    act(v("xt", 4 * lo + b, 4 * hi, 4), x32, 0.03125)
-                else:
-                    ts(v("xt", 4 * lo + b, 4 * hi, 4), x32, 0.03125, Alu.mult)
-            quant(v("qx", lo, hi), v("sx", lo, hi), v("xt", 4 * lo, 4 * hi))
+                tt(v("x32", *at4), bank(at + b, n), v("z32", *at4), Alu.add)
+                times(TUNE["xs"][at + b], v("xt", *at4), v("x32", *at4), 0.03125)
+            quant(v(nq, lo, hi), v(ns, lo, hi), v("xt", 4 * lo, 4 * hi))
 
-    for lo, at, q in ((0, 0, "S"), (H, 4, "Y")):
-        mm(at, "qv", "sv", 0, "qx", "sx", lo, H)
-        (cp if lo else act)(v("yt", lo, lo + H), bank(at, H))
-        store(q, T.y[:, lo:lo + H], T.yt[:, lo:lo + H], v("yt", lo, lo + H)[1])
-        store("Y", T.oc[:, 4 * lo:4 * (lo + H)], T.qx[:, lo:lo + H].bitcast(dt.uint8), v("qx", lo, lo + H)[1])
+    for i, (lo, hi, at) in enumerate(parts):
+        mm(at, "qv", "sv", 0, "qx", "sx", lo, hi - lo)
+        times("SV"[i % 2], v("yt", lo, hi), bank(at, hi - lo))
+        store("SY"[i % 2], T.y[:, lo:hi], T.yt[:, lo:hi], v("yt", lo, hi)[1])
+        store("Y", T.oc[:, 4 * lo:4 * hi], T.qx[:, lo:hi].bitcast(dt.uint8), v("qx", lo, hi)[1])
     for k in range(4):
         store("SY"[k % 2], T.osc[4 * k:4 * k + 4, :], T.sx[32 * k:32 * k + 4, :], v("sx")[1])
 

@@ -37,41 +37,44 @@ _buf("qx qz lx0 lx1 lx2 qe0 qe1 qe2 qo0 qo1 qo2", C, F8)
 _buf("sx sz ls0 ls1 ls2 se0 se1 se2 so0 so1 so2", C, U8)
 _buf("qd qde qdo qw", 512, F8)
 _buf("sd sde sdo sw", 512, U8)
-_buf("qu qur qv", 128, F8)
-_buf("su sur sv", 128, U8)
+_buf("qu qv", 128, F8)
+_buf("su sv", 128, U8)
+_buf("qur", 256, F8)
+_buf("sur", 256, U8)
+_buf("wt0 wt1 wt2 wt3", 2 * C, BF)
+_buf("fh0 fh1 fh2 fh3", C, BF)
 _buf("nodi pari", K, I32)
 _buf("pidx", 8, I32)
 _buf("half", 8, F32)
-_buf("uli", 8, F32)
-_buf("ulu", 8, U16)
+_buf("uli", 16, F32)
+_buf("ulu", 16, U16)
 _buf("nodu np0 np1 np2 og0 og1 og2 ol0 ol1 ol2", K, U16)
 _buf("yt opn", C, F32)
 _buf("ws0 ws1 ws2 wl0 wl1 wl2", K, BF)
-_pool("lf32", F32, ("cols ge gc lt", 16), ("two", 4), ("iota srcw", 2 * C), ("sab far near", 2 * K),
-      ("k16 k256 stc vm ownm owng t0 t1 t2 t3 t8 t9", K),
-      ("nodnr sc s1 f1 f2 inv1 sj sn nw0 nw1 nw2", C))
-_pool("lu16", U16, ("c15 d2u stu g0 g1 g2 g4 keyu o3u cgu of2 sju tu", K), ("pick", 64), ("invu", 2 * K))
-_pool("lbf", BF, ("selg jt16 diag thr d2 d4 d8 db c2 c4 c8 pa pb pc pd siz lsc sel0 "
+_pool("lf32", F32, ("cols ge gc lt", 16), ("two", 4), ("iota srcw", 2 * C), ("sab ends far near", 2 * K),
+      ("k16 k256 stc vm ownm owng link t0 t1 t2 t9", K), ("sc", 2 * C),
+      ("nodnr s1 f1 f2 inv1 sj sn nw0 nw1 nw2", C))
+_pool("lu16", U16, ("noda nodb mine inv0 d2u stu g0 g1 g2 g4 keyu posu o3u cgu of2 sju tu", K), ("pick", 64), ("invu", 2 * K))
+_pool("lbf", BF, ("selg jt16 thr d2 d4 d8 db c2 c4 c8 pa pb pc pd siz lsc sel0 "
                   "dif cmpm stn stl xx spk nbk cmk pos g3c wc1 eq asum won lj rmp rs dtu dng "
-                  "yq hh stsc", C), ("mx sell", 2 * C),
-      ("jt keep ta tb selw", C + 16), ("ab", C + 64), ("wdec", 2 * C + 2), ("valt tw3 tw2 ktab", 256), ("xtab", 16))
-_pool("lf16", F16, ("h2 h4 oh osum spc nbc dse seen trn inv2", C), ("cw dl", 2 * C))
+                  "yq hh stsc", C), ("mx", 2 * C),
+      ("jt keep diag ta tb selw", C + 16), ("ab", C + 64), ("wdec", 2 * C + 2), ("valt valt2 tw2 ktab", 256), ("xtab turn", 16))
+_pool("lf16", F16, ("h2 h4 oh osum spc nbc dse seen trn inv2", C), ("cw dl dm", 2 * C))
 SCRATCH["ps"] = ("psum", [128, 4096], F32)
 PLACE["ps"] = ("ps", 0, 4096)
 
-LOADS = ["dx", "dnod", "dpar", "du", "dwc", "dws", "dv", "dz"]
+LOADS = ["dx", "dnod", "dpar", "du", "dwc", "dws", "dv", "dz", "dh0", "dh1", "dh2", "dh3"]
 SEMAPHORES = (["qV", "qS", "qP", "qG", "sent", "stored"] + LOADS
               + ["%s%d" % (n, r) for n in ("an", "ax", "as", "ao", "av", "aw") for r in range(3)])
 
 Alu = AluOpType
 Act = ActivationFunctionType
-PACES = [dict(c=0.00085, t=0.0010, g=0.0012, p=0.0006, call=0.5, same=0.24, wake=0.24, psum=0.0, word=1.3, big=6.0,
-              first=9.0, each=0.0),
-         dict(c=0.00094, t=0.0018, g=0.0010, p=0.0008, call=0.45, same=0.22, wake=0.22, psum=0.0, word=2.1, big=7.0,
+PACES = [dict(c=0.00099, t=0.0016, g=0.0012, p=0.0009, call=0.7, same=0.227, wake=0.227, psum=0.0, word=2.1, big=7.0,
               first=10.0, each=0.0)]
-TUNE = dict(paces=PACES, ex=(0, 4), es=(0, 4), ew=(0, 4), eo=(0, 4), look=0.3, seed=3, turns=10000, slack=0.08, skew=0.0,
-            cut=192, copy="SS", td=(2, 1), whole=0, ft="SSSS", z="SSSVSSSV", z32="SSVVSSVV", xs="SSSSSSSV",
-            g3c="VS", ab="VS", sn="VS", cw="VS", sc="S", t1=2, t2=2, t4=2, t5=1,
+TUNE = dict(paces=PACES, ex=(0, 4), es=(0, 4), ew=(0, 4), eo=(0, 4), look=0.7, tries=300, just=20, noise=2.0, seed=1, turns=5000, slack=0.08, skew=0.0, spare=-3.0,
+            cut=((224,), (224,), (224,)), copy="SSSS", early="VV", wide=0, free=0, twice=0, late8=0, packed=(0, 0, 0), td=(2, 2), whole=0, ft="SSSS",
+            z=("SSSVSSSV",) * 2, z32=("SSSSSSSS", "SSSSSSSS"), xs=("SSSSSSSV",) * 2,
+            g3c="VS", ab="VS", sn="VS", cw="SVS", sc="SSSVSV", f1="VS", later=-8.0, double=0.0, t1=2, t2=2, t4=2, t5=1,
             nbk="V", nbc="V", ws="V", words=1)
 ORDER = {}
 
@@ -84,7 +87,7 @@ def _meet(a, b):
 
 def _order(ops, queues):
     n = len(ops)
-    before = [sorted(o["need"]) for o in ops]
+    before = [sorted(o["need"] | o["behind"]) for o in ops]
     after = [[] for _ in ops]
     for i in range(n):
         for j in before[i]:
@@ -93,7 +96,7 @@ def _order(ops, queues):
     for pace in TUNE["paces"]:
         late_ = [pace.get(o["late"], o["late"]) for o in ops]
         plans.append(([pace["each"] + o["cost"][1] + pace[o["cost"][0]] * o["cost"][2] for o in ops], late_,
-                      [[(j, 0.0 if ops[i]["q"] == ops[j]["q"] == "P" else
+                      [[(j, 0.0 if ops[i]["q"] == ops[j]["q"] == "P" or j not in ops[i]["need"] else
                          late_[j] + pace["same" if ops[i]["q"] == ops[j]["q"] else "wake"]) for j in before[i]]
                        for i in range(n)]))
     cost, late, links = plans[0]
@@ -102,25 +105,29 @@ def _order(ops, queues):
     def lag(i, j):
         return delay[i, j]
 
-    def lay(rank_):
+    def lay(rank_, look):
         left = [len(p) for p in before]
         ready = [0.0] * n
         free = {q: 0.0 for q in queues}
         mine = {q: [i for i in range(n) if not left[i] and ops[i]["q"] == q] for q in queues}
         at = [0.0] * n
+        choice, stale = {}, set(queues)
         for _ in range(n):
-            best = None
-            for q, m in mine.items():
+            for q in stale:
+                m = mine[q]
+                choice.pop(q, None)
                 if m:
                     t = max(free[q], min(ready[i] for i in m))
                     i = min((i for i in m if ready[i] <= t + 0.02), key=lambda i: rank_[i])
-                    soon = [j for j in m if rank_[j] < rank_[i] and ready[j] < t + TUNE["look"] * cost[i]]
+                    soon = [j for j in m if rank_[j] < rank_[i] and ready[j] < t + cost[i]]
                     if soon:
-                        i = min(soon, key=lambda j: rank_[j])
-                    s = max(free[q], ready[i])
-                    if best is None or s < best[0]:
-                        best = (s, i)
-            s, i = best
+                        j = min(soon, key=lambda j: rank_[j] + ready[j])
+                        if (max(ready[j] - rank_[j], ready[j] + cost[j] - rank_[i]) + look[j] * (ready[j] - t)
+                                < t + cost[i] - rank_[j]):
+                            i = j
+                    choice[q] = (max(free[q], ready[i]), i)
+            s, i = min(choice.values())
+            stale = {ops[i]["q"]}
             at[i] = s
             free[ops[i]["q"]] = s + cost[i]
             mine[ops[i]["q"]].remove(i)
@@ -129,18 +136,22 @@ def _order(ops, queues):
                 left[j] -= 1
                 if not left[j]:
                     mine[ops[j]["q"]].append(j)
+                    stale.add(ops[j]["q"])
         return at
 
     way = [0.0] * n
     for i in range(n - 1, -1, -1):
         way[i] = cost[i] + max([way[j] + lag(i, j) for j in after[i]] + [late[i]])
+    ORDER["bound"] = (max(way), {q: round(sum(c for c, o in zip(cost, ops) if o["q"] == q), 1) for q in queues})
     seed = [TUNE["seed"]]
 
     def draw(m):
         seed[0] = (seed[0] * 6364136223846793005 + 1442695040888963407) % 2 ** 64
         return (seed[0] >> 33) % m
 
-    at = lay([-w - o["ahead"] for w, o in zip(way, ops)])
+    rank_ = [-w - o["ahead"] for w, o in zip(way, ops)]
+    look = [TUNE["look"]] * n
+    at = lay(rank_, look)
     line = sorted(range(n), key=lambda i: (at[i], i))
     queue = [o["q"] for o in ops]
 
@@ -171,18 +182,79 @@ def _order(ops, queues):
         for (cost_, late_, _), (end, held) in zip(plans, state):
             i = max(range(n), key=lambda k: end[k] + late_[k])
             while held[i] >= 0:
-                if held[i] not in ops[i]["need"]:
+                if held[i] not in before[i]:
                     found.append((held[i], i))
                 i = held[i]
         return found
 
-    best, state = play(line, 0, [([0.0] * n, [-1] * n) for _ in plans])
-    found, now, keep = waits(state), best, line
+    def tails(line_):
+        out = []
+        for cost_, late_, links_ in plans:
+            rest, nxt = list(late_), {}
+            for i in line_[::-1]:
+                t = rest[i] = cost_[i] + max(rest[i], nxt.get(queue[i], 0.0))
+                nxt[queue[i]] = t
+                for j, d in links_[i]:
+                    if rest[j] < t + d:
+                        rest[j] = t + d
+            out.append(rest)
+        return out
+
+    def least(line_, a, b, old, rests):
+        total, span = 0.0, line_[a:b + 1]
+        inside, prev0, nxt = set(span), {}, {}
+        for i in line_[a - 1::-1] if a else ():
+            prev0.setdefault(queue[i], i)
+            if len(prev0) == len(queues):
+                break
+        for i in line_[b + 1:]:
+            nxt.setdefault(queue[i], i)
+            if len(nxt) == len(queues):
+                break
+        for (cost_, late_, links_), (end, _), rest, out in zip(plans, old, rests, onward):
+            free = {q: end[i] for q, i in prev0.items()}
+            new, most = {}, 0.0
+            for i in span:
+                t = free.get(queue[i], 0.0)
+                for j, d in links_[i]:
+                    t = max(t, new.get(j, end[j]) + d)
+                t = new[i] = free[queue[i]] = t + cost_[i]
+                for k, d in out[i]:
+                    if k not in inside:
+                        most = max(most, t + d + rest[k])
+            total += max([most] + [free[q] + rest[i] for q, i in nxt.items() if q in free])
+        return total
+
+    onward = [[[] for _ in ops] for _ in plans]
+    for out, (_, _, links_) in zip(onward, plans):
+        for i in range(n):
+            for j, d in links_[i]:
+                out[j].append((i, d))
+    twins = {}
+    for i, o in enumerate(ops):
+        twins.setdefault(o["role"], []).append(i)
+    blank = [([0.0] * n, [-1] * n) for _ in plans]
+    best, state = play(line, 0, blank)
+    for _ in range(TUNE["tries"]):
+        new = list(rank_) if draw(100) >= TUNE["just"] else [-sum(r_) / len(plans) for r_ in zip(*tails(line))]
+        for _ in range(draw(7)):
+            i, d = draw(n), (draw(100) - 50) * TUNE["noise"] / 100
+            for k in twins[ops[i]["role"]] if draw(2) else [i]:
+                for j in [k] + (before[k] if d < 0 else after[k]):
+                    new[j] += d
+        i, patience = draw(n), list(look)
+        patience[i:i + 60] = [draw(9) / 4] * len(look[i:i + 60])
+        at = lay(new, patience)
+        laid = sorted(range(n), key=lambda i: (at[i], i))
+        total, tried = play(laid, 0, blank)
+        if total <= best:
+            best, state, line, rank_, look = total, tried, laid, new, patience
+    found, now, keep, rests = waits(state), best, line, tails(line)
     for turn in range(TUNE["turns"]):
         p, i = found[draw(len(found))]
         a, b = line.index(p), line.index(i)
         early = draw(2)
-        for _ in range(draw(3)):
+        for _ in range(draw(3) if draw(4) else draw(16)):
             if early:
                 a = next((k for k in range(a - 1, -1, -1) if queue[line[k]] == queue[i]), a)
             else:
@@ -196,10 +268,14 @@ def _order(ops, queues):
             continue
         go, stay = [k for k in span if k in moved], [k for k in span if k not in moved]
         new = line[:a] + (go + stay if early else stay + go) + line[b + 1:]
+        bound = now + TUNE["slack"] * (1 - turn / TUNE["turns"]) * draw(100) / 100
+        if least(new, a, b, state, rests) > bound:
+            continue
         total, tried = play(new, a, state)
-        if total <= now + TUNE["slack"] * (1 - turn / TUNE["turns"]) * draw(100) / 100:
-            line, now, state = new, total, tried
-            found = waits(state)
+        if total <= bound:
+            now, state = total, tried
+            line = sorted(new, key=lambda k: state[0][0][k] - cost[k])
+            found, rests = waits(state), tails(line)
             if now < best:
                 best, keep = now, line
     ORDER["end"] = best / len(plans)
@@ -214,6 +290,7 @@ def rank_program(g, core, T, topo):
     ops = []
     acc = {}
     ahead = [0.0]
+    gate = []
 
     def v(name, a=0, b=None, s=1):
         buf, at, n = PLACE[name]
@@ -263,7 +340,9 @@ def rank_program(g, core, T, topo):
                     if (wr or a[1] or (name == "ps" and a[2] != q)) and _meet(run_, a[0]):
                         need.add(a[3])
         me = len(ops)
-        ops.append(dict(q=q, issue=issue, need=need, cost=cost, late=late, sem=sem or "q" + q, inc=inc, ahead=ahead[0]))
+        ops.append(dict(q=q, issue=issue, need=need, cost=cost, late=late, sem=sem or "q" + q, inc=inc, ahead=ahead[0],
+                        behind={j for j in gate if ops[j]["q"] == q},
+                        role=(q,) + tuple((name.rstrip("012"), r_) for name, r_ in writes[:1] + list(reads[:1]))))
         for name, r_ in writes:
             acc[name] = [a for a in acc.get(name, []) if not (
                 r_[0] <= a[0][0] and a[0][1] <= r_[1] and (r_[2] == 1 or (r_[2] == a[0][2] and _meet(r_, a[0]))))]
@@ -367,17 +446,18 @@ def rank_program(g, core, T, topo):
     reach = [k for k in topo.engines(core, peer(0)) if all(k in topo.engines(core, peer(j)) for j in range(3))]
 
     def send(dst, land, src, sem, late, share):
-        e_ = reach[len(reach) * share[0] // 4:len(reach) * share[1] // 4]
+        all_ = topo.engines(core, dst) if TUNE["wide"] else reach
+        e_ = all_[len(all_) * share[0] // 4:len(all_) * share[1] // 4]
         rid, pid, _ = topo.addr(dst)
         sent[0] += len(e_)
         add("G", lambda: g.remote_dma(land[0], src[0], T.sem[sem], T.sem.sent, pid, rid, sum(1 << k for k in e_)),
             src[1], land[1], ("call", 0.0, 1), late, (sem,), len(e_))
 
-    PM, CA, CB, ST, I16, GL, E15B = range(7)
+    PM, CA, CB, ST, SN, I16, GL, E15B = range(8)
     GE6, E15, LT6, LT14, LT15 = col(6, "ge"), col(15, "ge"), col(6, "lt"), col(14, "lt"), col(15, "lt")
-    parts = [(0, TUNE["cut"], 0), (TUNE["cut"], C, 4)]
+    cuts = [[(lo, hi, 4 * (i % 2)) for i, (lo, hi) in enumerate(zip((0,) + c, c + (C,)))] for c in TUNE["cut"]]
 
-    load("Y", "dx", v("x0"), T.x[:], 3.2)
+    load("Y", "dx", v("x0"), T.x[:], 3.7)
     load("S", "dpar", v("pari"), T.par[:], 2.1)
     load("S", "dnod", v("nodi"), T.nod[:], 2.1)
     load("S", "du", v("ut"), T.u[:], 2.6)
@@ -392,12 +472,13 @@ def rank_program(g, core, T, topo):
     total(v("jt"), v("keep"))
     iota(v("k16"), [[16, K]])
     iota(v("k256"), [[256, K]])
-    iota(v("uli"), [[16, 8]])
+    iota(v("uli"), [[16, 2], [32, 4], [0, 2]])
     iota(v("iota", 0, C), [[1, C]])
     iota(v("valt"), [[1, 16], [0, 16]])
     iota(v("idn"), [[1, 128]], 0, -1)
-    iota(v("ktab"), [[16, 256]])
-    iota(v("xtab"), [[256, 16]])
+    iota(v("valt2"), [[1, 256]])
+    act(v("ktab"), v("valt2"), 512.0)
+    iota(v("xtab"), [[8192, 16]])
     for name, c in (("spk", 0), ("rmp", -1), ("dtu", 1), ("dng", 1)):
         iota(v(name), [[0, C]], c)
     iota(v("wdec", 0, 2 * C + 2, 2), [[0, C + 1]], -1)
@@ -405,47 +486,52 @@ def rank_program(g, core, T, topo):
     ts(v("pidx", 1, 2), v("pidx", 0, 1), 15, Alu.bitwise_and)
     ts(v("pidx", 2, 3), v("pidx", 0, 1), 16, Alu.bitwise_and)
     cp(col(PM), v("pidx", 1, 2))
-    ts(col(0, "half"), v("pidx", 2, 3), 0.0, Alu.is_equal)
-    ts(col(1, "half"), v("pidx", 2, 3), 0.0, Alu.is_gt)
+    ts(col(1, "half"), v("pidx", 2, 3), C / 16, Alu.mult)
     ts(v("ge"), v("jt", 0, 16), col(PM), Alu.is_le)
     ts(v("gc"), v("jt", 0, 16), col(PM), Alu.is_le, float(C), Alu.mult)
     ts(v("lt"), v("jt", 0, 16), col(PM), Alu.is_gt)
     act(col(I16), col(PM), 16.0)
     act(col(ST), LT15, 1024.0)
-    act(col(CA), LT15, 2.0, col(PM))
-    act(col(CB), LT15, 1.0, 14.0)
-    act(col(E15B), E15, 2000.0)
     act(col(GL), col(1, "lt"), 8192.0, -1024.0)
     act(v("jt16"), jt, 16.0)
-    ts(w("diag"), jt, col(PM), Alu.is_equal)
-    ts(v("ta"), v("jt"), col(PM), Alu.is_equal, -8192.0, Alu.mult)
-    act(v("tb"), v("ta"), 2.0 ** -16)
+    ts(v("diag"), v("jt"), col(PM), Alu.is_equal)
+    act(v("ta"), v("diag"), -8192.0)
+    act(v("tb"), v("diag"), -0.125)
     scan(v("selw", 0, C + 1), v("tb", 15, C + 16), v("ta", 0, C + 1), Alu.mult, Alu.add)
     act(v("selg"), v("selw", 1, C + 1))
     tt(last("selg"), last("selg"), v("k256"), Alu.add)
-    ts(v("c15"), v("k16"), 15.0, Alu.add)
-    ts(v("thr"), jt, col(PM), Alu.is_lt, 2.0 ** -110, Alu.mult)
-    ts(v("tw3"), v("jt", 0, 256), 1.0, Alu.add, col(CA), Alu.is_equal)
-    tt(v("tw3"), v("tw3"), v("valt"), Alu.mult)
+    ts(v("thr"), jt, col(PM), Alu.is_lt, -2.0 ** -110, Alu.mult)
     ts(v("tw2"), v("valt"), col(PM), Alu.is_equal)
     tt(v("tw2"), v("tw2"), v("diag", 0, 256), Alu.max)
-    ts(v("spc"), jt, 0.0, Alu.mult)
-    act(last("dtu"), v("k16"), -1.0, -128.0)
-    act(last("dng"), v("k16"), 0.0, -1.0)
-    act(v("dse"), w("diag"), -1024.0)
-    act(last("dse"), v("k16"), 0.0, -1024.0)
+    iota(last("dtu"), [[-16, K]], -128)
+    iota(last("dng"), [[0, K]], -1)
+
+    def middle_constants():
+        act(col(SN), LT15, 1024.0, 15 * 8192.0)
+        act(col(CA), LT15, 2.0, col(PM))
+        act(col(CB), LT15, 1.0, 14.0)
+        act(col(E15B), E15, 2000.0)
+        ts(v("turn"), v("jt", 0, 16), 1.0, Alu.add, col(CA), Alu.is_equal)
+        act(v("spc"), jt, 0.0)
+        act(v("dse"), w("diag"), -1024.0)
+        act(last("dse"), v("k16"), 0.0, -1024.0)
+        ts(col(0, "half"), v("pidx", 2, 3), 0.0, Alu.is_equal)
+        ts(col(2, "half"), v("pidx", 2, 3), 0.0, Alu.is_gt)
+        unpackers("qd", "sd", 1.0)
+
     ts(v("idn"), v("idn"), 0.0, Alu.is_equal)
     fill(v("et", 0, 1024), 0.0)
     load("Y", "dz", v("et", 1024, 2048), T.et[:, 0:1024], 2.3, v("et", 0, 1024)[1])
-    for q, s, m in (("qd", "sd", 1.0), ("qde", "sde", col(0, "half")), ("qdo", "sdo", col(1, "half"))):
+
+    def unpackers(q, s, m):
         for b in range(4):
             act(v("et", 512 * b + b, 512 * (b + 1), 4), v("idn"), m)
-        quant(v(q), v(s), v("et"))
+            quant(v(q, 128 * b, 128 * b + 128), v(s, 128 * b, 128 * b + 128), v("et", 512 * b, 512 * (b + 1)))
+
     cp(v("ulu"), v("uli"))
     quant(v("qu"), v("su"), v("ut"))
     cp(bits(v("qur"), dt.uint32), ind(bits(v("qu"), dt.uint32), v("ulu")))
     act(v("sur"), ind(v("su"), v("ulu")))
-    quant(v("qv"), v("sv"), v("vt"))
 
     def glob(out, tmp, loc, off=None):
         tt(v(tmp), loc, v("k256"), Alu.add)
@@ -476,107 +562,147 @@ def rank_program(g, core, T, topo):
         v("np0")[1] + v("np1")[1] + v("np2")[1], ("call", 0.0, 1), "first", ("an0", "an1", "an2"), n)
     ahead[0] = 0.0
     act(v("nodnr"), ind(v("iota", 0, C), v("nodu")))
-    run("V", g.vector.tensor_copy, (ind(v("inv1"), v("nodu"))[0], v("inv1")[1]), [v("iota", 0, C)], ("g", 0.05, 2 * C),
-        reads=[v("nodu")])
-    diagonal(v("inv2"), v("inv1"))
+    ts(v("noda"), v("nodi"), col(1, "half"), Alu.add)
+    turn(v("s1"), v("nodnr"))
     for o in (0, 1):
-        ts(v("invu", o, 2 * K, 2), last("inv2"), col(ST), Alu.subtract)
+        ts(v("nodb", o, K, 2), v("s1", 16 * o, C, 32), float(C * o), Alu.add)
+
+    def late_constants():
+        for p in runs(2):
+            run("V", g.vector.tensor_copy, (ind(v("inv1"), sh("nodu", p))[0], v("inv1")[1]), [wd("iota", p)],
+                ("g", 0.05, C), reads=[v("nodu"), v("inv1")] if p[0] else [v("nodu")])
+        for p in runs(2):
+            diagonal(wd("inv2", p), wd("inv1", p))
+        if min(TUNE["packed"]) == 0:
+            ts(v("inv0"), last("inv2"), col(ST), Alu.subtract)
+        if max(TUNE["packed"]):
+            for o in (0, 1):
+                ts(v("invu", o, 2 * K, 2), last("inv2"), col(ST), Alu.subtract)
+            unpackers("qde", "sde", col(0, "half"))
+            unpackers("qdo", "sdo", col(2, "half"))
+        quant(v("qv"), v("sv"), v("vt"))
 
     ts(v("g0"), v("pari"), 16.0, Alu.mult, col(PM), Alu.add)
     ts(first("spk"), v("pari"), col(I16), Alu.add)
-    total(v("nbk"), v("spk"))
-    tt(v("cmk"), ind(v("iota", 0, 256), v("g0")), v("nbk"), Alu.is_equal)
-    total(v("pos"), v("cmk"))
     ts(v("t1"), v("pari"), col(PM), Alu.subtract, 0.0, Alu.max)
     cp(v("t2"), v("pari"))
     tt(v("t0"), v("t2"), v("k16"), Alu.add)
-    tt(v("t1"), v("t1"), last("pos"), Alu.mult)
-    tt(v("t0"), v("t0"), v("t1"), Alu.subtract)
-    tt(v("t2"), v("t2"), v("t1"), Alu.subtract)
-    cp(v("g1"), v("t0"))
-    ts(v("d2u"), v("t2"), 16.0, Alu.mult, col(PM), Alu.add)
-    act(v("pa"), ind(v("jt16"), v("g1")))
+    for p in runs(TUNE["td"][0]):
+        total(wd("nbk", p), wd("spk", p))
+        tt(wd("cmk", p), ind(v("valt2"), sh("g0", p)), wd("nbk", p), Alu.is_equal)
+        total(wd("pos", p), wd("cmk", p))
+        tt(sh("t1", p), sh("t1", p), last("pos", p), Alu.mult)
+        tt(sh("link", p), sh("t0", p), sh("t1", p), Alu.subtract)
+        tt(sh("t2", p), sh("t2", p), sh("t1", p), Alu.subtract)
+        cp(sh("g1", p), sh("link", p))
+        ts(sh("d2u", p), sh("t2", p), 16.0, Alu.mult, col(PM), Alu.add)
+        times(TUNE["early"][0] if p[0] else "S", wd("pa", p), ind(v("jt16"), sh("g1", p)))
+    gate[:] = [len(ops) - 3]
     quant(v("qb0", 0, C), v("sb0", 0, C), v("x0"))
+    gate[:] = []
 
     for r in range(3):
         to = peer(r)
-        final = r == 2
+        final, parts, packed = r == 2, cuts[r], TUNE["packed"][r]
         qb, sb, lx, ls, qe, se, qo, so, og, ol, ws, wl, nw = (
             n + str(r) for n in ("qb", "sb", "lx", "ls", "qe", "se", "qo", "so", "og", "ol", "ws", "wl", "nw"))
         send(to, bits(v(lx), dt.uint8), bits(v(qb, 0, C), dt.uint8), "ax%d" % r, "big" if r else "first", TUNE["ex"])
         send(to, v(ls), v(sb, 0, C), "as%d" % r, "big" if r else "first", TUNE["es"])
         for p in runs(TUNE["td"][r > 0]):
-            act(wd("pb", p), ind(upto("pa", p), sh("g1", p)))
+            times("S" if r or not p[0] else TUNE["early"][1], wd("pb", p), ind(upto("pa", p), sh("g1", p)))
             act(wd("d2", p), ind(v("tw2"), sh("d2u", p)), 2.0, -1.0)
-            times(TUNE["copy"][0], wd("c2", p), wd("d2", p))
+            times(TUNE["copy"][2 * (r > 0)], wd("c2", p), wd("d2", p))
             places("g2", "h2", "pb", p)
             act(wd("pc", p), ind(upto("pb", p), sh("g2", p)))
             tt(wd("d4", p), ind(upto("d2", p), sh("g2", p)), wd("c2", p), Alu.max)
-            times(TUNE["copy"][1], wd("c4", p), wd("d4", p))
+            times(TUNE["copy"][2 * (r > 0) + 1], wd("c4", p), wd("d4", p))
             places("g4", "h4", "pc", p)
             tt(wd("d8", p), ind(upto("d4", p), sh("g4", p)), wd("c4", p), Alu.max)
+        if r == 0:
+            gate[:] = [len(ops) - 4, len(ops) - 1]
+            middle_constants()
+            gate[:] = []
+        for i, (lo, hi, _) in enumerate(cuts[r - 1] if r else [(0, C, 0)]):
+            for o in (0, 1):
+                mm(2 * i + o, "qur", "sur", o, qb, sb, lo, hi - lo)
+                times(TUNE["sc"][2 * i + o], v("sc", C * o + lo, C * o + hi), bank(2 * i + o, hi - lo))
+        for p in runs(TUNE["t1"]):
+            gather(TUNE["f1"], "f1", 0, v("sc"), "nodb", p)
+        gate_ = [len(ops) - 1] if r and TUNE["late8"] else []
+        for p in runs(TUNE["td"][r > 0]):
+            gate[:] = gate_ if p[0] or TUNE["late8"] > 1 else []
             act(wd("c8", p), ind(upto("d8", p), sh("g4", p)))
+            gate[:] = []
             tt(wd("db", p), ind(upto("c8", p), sh("g4", p)), wd("d8", p), Alu.max)
             total(wd("siz", p), wd("db", p))
-        for i, (lo, hi, _) in enumerate(parts if r else [(0, C, 0)]):
-            mm(i, "qur", "sur", 0, qb, sb, lo, hi - lo)
-            times(TUNE["sc"], v("sc", lo, hi), bank(i, hi - lo))
         for p in runs(TUNE["t1"]):
-            act(wd("s1", p), ind(v("sc"), sh("nodu", p)))
-            tt(wd("f1", p), ind(v("sc"), sh("nodu", p)), wd("diag", p), Alu.mult)
-            total(wd("f2", p), wd("f1", p))
-            tt(wd("dif", p), ind(upto("f2", p), sh("c15", p)), wd("s1", p), Alu.subtract)
-            tt(wd("cmpm", p), wd("dif", p), wd("thr", p), Alu.is_lt)
+            turn(wd("f2", p), wd("f1", p))
+            tt(wd("dif", p), ind(v("sc"), sh("noda", p)), wd("f2", p), Alu.subtract)
+            tt(wd("cmpm", p), wd("dif", p), wd("thr", p), Alu.is_gt)
             total(wd("stsc", p), wd("cmpm", p))
             ts(sh("stu", p), last("stsc", p), 0.0, Alu.add)
         act(v("stc"), last("stsc"), 1.0, -16.5)
         act(first("rmp"), last("stsc"), 1.0, -0.5)
+        gate_ = []
         for p in runs(TUNE["t2"]):
-            ahead[0] = 0.0 if p[0] else TUNE["skew"]
             both = (2 * p[0], 2 * p[1])
             low, high = (2 * p[0], p[0] + p[1]), (p[0] + p[1], 2 * p[1])
-            act(sh("sab", low), last("siz", p), 8.0, 128.0)
-            act(sh("sab", high), last("siz", p), -8.0, 128.0)
-            act(last("sell", low), last("stsc", p), 16.0, col(ST))
-            act(wd("stn", p), ind(v("jt16", 0, 16), sh("stu", p)))
-            act(wd("stl", p), ind(upto("stn", p), sh("g1", p)))
+            act(sh("sab", low), last("siz", p), 256.0, 4096.0)
+            act(sh("sab", high), last("siz", p), -256.0, 4096.0)
+            if r == 0:
+                ts(sh("ends", low), sh("k256", p), col(I16), Alu.add, col(ST), Alu.add)
+                act(sh("ends", high), sh("link", p), 16.0, col(ST))
+            act(wd("stn", p), ind(v("jt", 0, 16), sh("stu", p)))
             tt(wd("xx", p), ind(v("xtab"), sh("stu", p)), wd("db", p), Alu.mult)
             scan(wd("mx", low), wd("keep", p), wd("xx", p), Alu.mult, Alu.max)
             scan(wd("mx", high), wd("xx", p), wd("dng", p), Alu.min, Alu.mult)
             tt(sh("far", both), last("mx", both), sh("sab", both), Alu.add)
             tt(first("spk", p), sh("far", low), sh("far", high), Alu.min)
             total(wd("nbk", p), wd("spk", p))
-            ts(sh("keyu", p), first("spk", p), 0.0625, Alu.mult)
+            ts(sh("keyu", p), first("spk", p), 2.0 ** -9, Alu.mult)
             tt(wd("cmk", p), ind(v("ktab"), sh("keyu", p)), wd("nbk", p), Alu.is_lt)
             total(wd("pos", p), wd("cmk", p))
-            diagonal(wd("sell", high), wd("stl", p))
-            tt(sh("near", both), last("mx", both), last("sell", both), Alu.add)
+            ts(sh("posu", p), last("pos", p), 0.0, Alu.add)
+            tt(sh("near", both), last("mx", both), sh("ends", both), Alu.add)
             tt(sh("vm", p), sh("near", low), sh("near", high), Alu.max)
-            tt(sh("t8", p), sh("vm", p), last("pos", p), Alu.add)
-            ts(sh("o3u", p), sh("t8", p), col(ST), Alu.subtract, 3840.0, Alu.subtract)
-            gather(TUNE["g3c"], "g3c", 0, v("tw3"), "o3u", p)
+            ts(sh("o3u", p), sh("vm", p), col(SN), Alu.subtract, 0.0625, Alu.mult)
+            act(wd("stl", p), ind(upto("stn", p), sh("o3u", p)))
+            tt(wd("g3c", p), ind(v("turn"), sh("posu", p)), wd("stl", p), Alu.mult)
             total(wd("wc1", p), wd("g3c", p))
             ts(sh(ws, p), last("wc1", p), GE6, Alu.mult, col(CB), Alu.min)
-        ahead[0] = 0.0
-        for i, p in enumerate(runs(TUNE["words"])):
-            send(to, sh(wl, p), sh(ws, p), "a%s%d" % ("wv"[i], r), "word", TUNE["ew"])
+            gate_.append(len(ops) - 1)
+        send(to, v(wl), v(ws), "aw%d" % r, "word", TUNE["ew"])
+        gate_.append(len(ops) - 1)
+        gate[:] = gate_[-1:] if TUNE["free"] else gate_
         tt(v("oh"), ind(v("diag", 0, 16), v("stu")), v("iota", 0, C), Alu.mult)
         total(v("osum"), v("oh"))
         ts(v(og), last("osum"), 0.0, Alu.add)
         send(to, v(ol), v(og), "ao%d" % r, "word", TUNE["eo"])
+        gate[:] = gate_
+        if r == 0:
+            late_constants()
         total(v("rs"), v("rmp"))
         ts(v("wdec", 1, 2 * C, 2), v("rs"), -1.0, Alu.max, 0.0, Alu.min)
         act(v("srcw", 0, C), ind(v("nodnr"), v(og)))
         act(v("won"), ind(v("jt16"), v(og)))
         act(v(nw), ind(v("iota", C, 2 * C), v("np%d" % r)))
         act(v("srcw", C, 2 * C), ind(v(nw), v(ol)))
-        for p in runs(TUNE["words"]):
-            act(sh("ownm", p), last("wc1", p), LT6)
-            tt(sh("owng", p), sh("ownm", p), sh("k16", p), Alu.add)
+        act(v("ownm"), last("wc1"), LT6)
+        tt(v("owng"), v("ownm"), v("k16"), Alu.add)
         for b in range(4):
             mm(4 + b, "qd", "sd", b, lx, ls)
             times(TUNE["ft"][b], v("ft", b, 4 * C, 4), bank(4 + b))
         quant(v(qb, C, 2 * C), v(sb, C, 2 * C), v("ft"))
+        gate[:] = []
+        for b in range(packed, 4):
+            mm(b, "qd", "sd", b, qb, sb)
+            act(v("wt%d" % b, 0, C), bank(b), 0.5)
+            if TUNE["twice"]:
+                act(v("fh%d" % b), bank(b), 0.5)
+            else:
+                load("Y", "dh%d" % b, v("fh%d" % b), v("wt%d" % b, 0, C)[0], 3.0, v("wt%d" % b, 0, C)[1])
+            mm(4 + b, "qd", "sd", b, qb, sb, C)
+            act(v("wt%d" % b, C, 2 * C), bank(4 + b), 0.5)
         for p in runs(TUNE["t4"]):
             at = 16 * (p[0] // (p[1] - p[0]))
             cg = first("spc", p)
@@ -600,44 +726,64 @@ def rank_program(g, core, T, topo):
         act(v("lj"), ind(v("won"), v("cgu")))
         if not final:
             act(last("lj"), last("won"))
-        for i, (lo, hi, _) in enumerate(parts):
+        for i, (lo, hi, _) in enumerate([] if packed else parts):
+            times(TUNE["cw"][i], v("cw", lo, hi), ind(v("sn"), v("inv0", lo // 16, hi // 16)))
+            gate_ = [len(ops) - 1]
+            diagonal(v("dm", lo, hi), v("cw", lo, hi))
+            ts(v("mine", lo // 16, hi // 16), v("dm", lo + 15, hi, 16), col(ST), Alu.subtract)
+        for i, (lo, hi, _) in enumerate(parts if packed else []):
             times(TUNE["cw"][i], v("cw", 2 * lo, 2 * hi), ind(v("sn"), v("invu", lo // 8, hi // 8)))
+            gate_ = [len(ops) - 1]
             turn(v("dl", 2 * lo, 2 * hi), v("cw", 2 * lo, 2 * hi))
             for o in (0, 1):
                 ts(v("pick", 32 * o + lo // 16, 32 * o + hi // 16), v("dl", 2 * lo + 16 * o, 2 * hi, 32), 0.0, Alu.add)
+            if packed < 4:
+                diagonal(v("dm", 2 * lo, 2 * hi), v("cw", 2 * lo, 2 * hi))
+                ts(v("mine", lo // 16, hi // 16), v("dm", 2 * lo + 15, 2 * hi, 32), col(ST), Alu.subtract)
         if final:
             act(v("opn"), ind(v("lj"), v("tu")), 0.0625)
             store("Y", T.op[:], T.opn[0:128:16, :], v("opn")[1])
         for p in [] if final else runs(TUNE["td"][1]):
+            gate[:] = gate_ if p[0] or TUNE["double"] else []
             act(wd("pa", p), ind(upto("lj", p), sh("tu", p)))
+            gate[:] = []
             diagonal(wd("lsc", p), wd("pa", p))
             ts(sh("d2u", p), last("lsc", p), col(ST), Alu.subtract, col(PM), Alu.add)
-            tt(sh("t9", p), last("lsc", p), sh("k256", p), Alu.add)
-            ts(sh("g1", p), sh("t9", p), col(ST), Alu.subtract, 0.0625, Alu.mult)
+            link = sh("ends", (p[0] + p[1], 2 * p[1]))
+            tt(link, last("lsc", p), sh("k256", p), Alu.add)
+            ts(sh("g1", p), link, col(ST), Alu.subtract, 0.0625, Alu.mult)
+        ahead[0] = 0.0
+        gate_ = []
         nq, ns = ("qx", "sx") if final else ("qb%d" % (r + 1), "sb%d" % (r + 1))
         for lo, hi, at in parts:
             n = hi - lo
-            for q, s, o in ((qe, se, 0), (qo, so, 32)):
+            for b in range(packed):
+                mm(at + b, "qd", "sd", b, qb, sb, lo, n, True, False)
+            for q, s, o, e_, es in ((qe, se, 0, "qde", "sde"), (qo, so, 32, "qdo", "sdo")) if packed else ():
+                gate[:] = gate_
                 off = v("pick", o + lo // 16, o + hi // 16)
                 cp(bits(v(q, lo, hi), dt.uint32), ind(bits(v(qb), dt.uint32), off))
                 act(v(s, lo, hi), ind(v(sb), off))
-            for b in range(4):
-                mm(at + b, "qd", "sd", b, qb, sb, lo, n, True, False)
-            for b in range(4):
-                mm(at + b, "qde", "sde", b, qe, se, lo, n, False, False)
-            for b in range(4):
-                mm(at + b, "qdo", "sdo", b, qo, so, lo, n, False, True)
-                times(TUNE["z"][at + b], v("zt", 4 * lo + b, 4 * hi, 4), bank(at + b, n), 0.5)
+                gate_ = [len(ops) - 2, len(ops) - 1]
+                for b in range(packed):
+                    mm(at + b, e_, es, b, q, s, lo, n, False, o > 0)
+                    gate_.append(len(ops) - 1)
+                gate[:] = []
+            for b in range(packed):
+                times(TUNE["z"][final][at + b], v("zt", 4 * lo + b, 4 * hi, 4), bank(at + b, n), 0.5)
+            for b in range(packed, 4):
+                tt(v("zt", 4 * lo + b, 4 * hi, 4), ind(v("wt%d" % b), v("mine", lo // 16, hi // 16)),
+                   v("fh%d" % b, lo, hi), Alu.add)
             quant(v("qz", lo, hi), v("sz", lo, hi), v("zt", 4 * lo, 4 * hi))
             if TUNE["whole"]:
                 times("V", v("z32", 4 * lo, 4 * hi), v("zt", 4 * lo, 4 * hi), 32.0)
             for b in range(4):
                 at4 = (4 * lo + b, 4 * hi, 4)
                 if not TUNE["whole"]:
-                    times(TUNE["z32"][at + b], v("z32", *at4), v("zt", *at4), 32.0)
+                    times(TUNE["z32"][final][at + b], v("z32", *at4), v("zt", *at4), 32.0)
                 mm(at + b, "qw", "sw", b, "qz", "sz", lo, n)
                 tt(v("x32", *at4), bank(at + b, n), v("z32", *at4), Alu.add)
-                times(TUNE["xs"][at + b], v("xt", *at4), v("x32", *at4), 0.03125)
+                times(TUNE["xs"][final][at + b], v("xt", *at4), v("x32", *at4), 0.03125)
             quant(v(nq, lo, hi), v(ns, lo, hi), v("xt", 4 * lo, 4 * hi))
 
     for i, (lo, hi, at) in enumerate(parts):

from concourse.bass import DstId, RemoteDMATransfer
from concourse.mybir import dt, AluOpType, ActivationFunctionType

C = 384
K = 24
H = C // 2
ROUNDS = (1, 2, 3)
F8, U8, BF, F16, F32, I32, U16 = "float8_e4m3fn_x4", "uint8", "bfloat16", "float16", "float32", "int32", "uint16"
SIZE = {F8: 4, U8: 1, BF: 2, F16: 2, F32: 4, I32: 4, U16: 2}

SCRATCH = {}
PLACE = {}


def _buf(names, cols, kind):
    for n in names.split():
        SCRATCH[n] = ("sbuf", [128, cols], kind)
        PLACE[n] = (n, 0, cols)


def _pool(pool, kind, *parts):
    at = 0
    for names, cols in parts:
        for n in names.split():
            PLACE[n] = (pool, at, cols)
            at += (cols + 15) // 16 * 16
    SCRATCH[pool] = ("sbuf", [128, at], kind)


_buf("x0 xt ft zt z32 x32", 4 * C, BF)
_buf("ut vt", 512, BF)
_buf("et", 2048, BF)
_buf("idn", 128, BF)
_buf("qb0 qb1 qb2", 2 * C, F8)
_buf("sb0 sb1 sb2", 2 * C, U8)
_buf("qx qz lx0 lx1 lx2 qe0 qe1 qe2 qo0 qo1 qo2", C, F8)
_buf("sx sz ls0 ls1 ls2 se0 se1 se2 so0 so1 so2", C, U8)
_buf("qd qde qdo qw", 512, F8)
_buf("sd sde sdo sw", 512, U8)
_buf("qu qv", 128, F8)
_buf("su sv", 128, U8)
_buf("qur", 256, F8)
_buf("sur", 256, U8)
_buf("wt0 wt1 wt2 wt3", 2 * C, BF)
_buf("fh0 fh1 fh2 fh3", C, BF)
_buf("nodi pari", K, I32)
_buf("pidx", 8, I32)
_buf("half", 8, F32)
_buf("uli", 16, F32)
_buf("ulu", 16, U16)
_buf("nodu np0 np1 np2 og0 og1 og2 ol0 ol1 ol2", K, U16)
_buf("yt opn", C, F32)
_buf("ws0 ws1 ws2 wl0 wl1 wl2", K, BF)
_pool("lf32", F32, ("cols ge gc lt", 16), ("two", 4), ("iota srcw", 2 * C), ("sab ends far near", 2 * K),
      ("k16 k256 stc vm ownm owng link t0 t1 t2 t9", K), ("sc", 2 * C),
      ("nodnr s1 f1 f2 inv1 sj sn nw0 nw1 nw2", C))
_pool("lu16", U16, ("noda nodb mine inv0 d2u stu g0 g1 g2 g4 keyu posu o3u cgu of2 sju tu", K), ("pick", 64), ("invu", 2 * K))
_pool("lbf", BF, ("selg jt16 thr d2 d4 d8 db c2 c4 c8 pa pb pc pd siz lsc sel0 "
                  "dif cmpm stn stl xx spk nbk cmk pos g3c wc1 eq asum won lj rmp rs dtu dng "
                  "yq hh stsc", C), ("mx", 2 * C),
      ("jt keep diag ta tb selw", C + 16), ("ab", C + 64), ("wdec", 2 * C + 2), ("valt valt2 tw2 ktab", 256), ("xtab turn", 16))
_pool("lf16", F16, ("h2 h4 oh osum spc nbc dse seen trn inv2", C), ("cw dl dm", 2 * C))
SCRATCH["ps"] = ("psum", [128, 4096], F32)
PLACE["ps"] = ("ps", 0, 4096)

LOADS = ["dx", "dnod", "dpar", "du", "dwc", "dws", "dv", "dz", "dh0", "dh1", "dh2", "dh3"]
SEMAPHORES = (["qV", "qS", "qP", "qG", "sent", "stored"] + LOADS
              + ["%s%d" % (n, r) for n in ("an", "ax", "as", "ao", "av", "aw") for r in range(3)])

Alu = AluOpType
Act = ActivationFunctionType
PACES = [dict(c=0.00099, t=0.0016, g=0.0012, p=0.0009, call=0.7, same=0.227, wake=0.227, psum=0.0, word=2.1, big=7.0,
              first=10.0, each=0.0)]
TUNE = dict(paces=PACES, ex=(0, 4), es=(0, 4), ew=(0, 4), eo=(0, 4), look=0.7, tries=300, just=20, noise=2.0, seed=1, turns=5000, slack=0.08, skew=0.0, spare=-3.0,
            cut=((224,), (224,), (224,)), copy="SSSS", early="VV", wide=0, free=0, twice=0, late8=0, packed=(0, 0, 0), td=(2, 2), whole=0, ft="SSSS",
            z=("SSSVSSSV",) * 2, z32=("SSSSSSSS", "SSSSSSSS"), xs=("SSSSSSSV",) * 2,
            g3c="VS", ab="VS", sn="VS", cw="SVS", sc="SSSVSV", f1="VS", later=-8.0, double=0.0, t1=2, t2=2, t4=2, t5=1,
            nbk="V", nbc="V", ws="V", words=1)
ORDER = {}


def _meet(a, b):
    if a[0] >= b[1] or b[0] >= a[1]:
        return False
    return a[2] != b[2] or (a[0] - b[0]) % a[2] == 0


def _order(ops, queues):
    n = len(ops)
    before = [sorted(o["need"] | o["behind"]) for o in ops]
    after = [[] for _ in ops]
    for i in range(n):
        for j in before[i]:
            after[j].append(i)
    plans = []
    for pace in TUNE["paces"]:
        late_ = [pace.get(o["late"], o["late"]) for o in ops]
        plans.append(([pace["each"] + o["cost"][1] + pace[o["cost"][0]] * o["cost"][2] for o in ops], late_,
                      [[(j, 0.0 if ops[i]["q"] == ops[j]["q"] == "P" or j not in ops[i]["need"] else
                         late_[j] + pace["same" if ops[i]["q"] == ops[j]["q"] else "wake"]) for j in before[i]]
                       for i in range(n)]))
    cost, late, links = plans[0]
    delay = {(j, i): d for i in range(n) for j, d in links[i]}

    def lag(i, j):
        return delay[i, j]

    def lay(rank_, look):
        left = [len(p) for p in before]
        ready = [0.0] * n
        free = {q: 0.0 for q in queues}
        mine = {q: [i for i in range(n) if not left[i] and ops[i]["q"] == q] for q in queues}
        at = [0.0] * n
        choice, stale = {}, set(queues)
        for _ in range(n):
            for q in stale:
                m = mine[q]
                choice.pop(q, None)
                if m:
                    t = max(free[q], min(ready[i] for i in m))
                    i = min((i for i in m if ready[i] <= t + 0.02), key=lambda i: rank_[i])
                    soon = [j for j in m if rank_[j] < rank_[i] and ready[j] < t + cost[i]]
                    if soon:
                        j = min(soon, key=lambda j: rank_[j] + ready[j])
                        if (max(ready[j] - rank_[j], ready[j] + cost[j] - rank_[i]) + look[j] * (ready[j] - t)
                                < t + cost[i] - rank_[j]):
                            i = j
                    choice[q] = (max(free[q], ready[i]), i)
            s, i = min(choice.values())
            stale = {ops[i]["q"]}
            at[i] = s
            free[ops[i]["q"]] = s + cost[i]
            mine[ops[i]["q"]].remove(i)
            for j in after[i]:
                ready[j] = max(ready[j], s + cost[i] + lag(i, j))
                left[j] -= 1
                if not left[j]:
                    mine[ops[j]["q"]].append(j)
                    stale.add(ops[j]["q"])
        return at

    way = [0.0] * n
    for i in range(n - 1, -1, -1):
        way[i] = cost[i] + max([way[j] + lag(i, j) for j in after[i]] + [late[i]])
    ORDER["bound"] = (max(way), {q: round(sum(c for c, o in zip(cost, ops) if o["q"] == q), 1) for q in queues})
    seed = [TUNE["seed"]]

    def draw(m):
        seed[0] = (seed[0] * 6364136223846793005 + 1442695040888963407) % 2 ** 64
        return (seed[0] >> 33) % m

    rank_ = [-w - o["ahead"] for w, o in zip(way, ops)]
    look = [TUNE["look"]] * n
    at = lay(rank_, look)
    line = sorted(range(n), key=lambda i: (at[i], i))
    queue = [o["q"] for o in ops]

    def play(line_, a, old):
        new, total = [], 0.0
        for (cost_, late_, links_), (end, held) in zip(plans, old):
            end, held = list(end), list(held)
            prev = {}
            for i in line_[a - 1::-1] if a else ():
                if queue[i] not in prev:
                    prev[queue[i]] = i
                    if len(prev) == len(queues):
                        break
            for i in line_[a:]:
                h = prev.get(queue[i], -1)
                t = end[h] if h >= 0 else 0.0
                for j, d in links_[i]:
                    if end[j] + d > t:
                        t, h = end[j] + d, j
                end[i], held[i] = t + cost_[i], h
                prev[queue[i]] = i
            total += max(e + d for e, d in zip(end, late_))
            new.append((end, held))
        return total, new

    def waits(state):
        found = []
        for (cost_, late_, _), (end, held) in zip(plans, state):
            i = max(range(n), key=lambda k: end[k] + late_[k])
            while held[i] >= 0:
                if held[i] not in before[i]:
                    found.append((held[i], i))
                i = held[i]
        return found

    def tails(line_):
        out = []
        for cost_, late_, links_ in plans:
            rest, nxt = list(late_), {}
            for i in line_[::-1]:
                t = rest[i] = cost_[i] + max(rest[i], nxt.get(queue[i], 0.0))
                nxt[queue[i]] = t
                for j, d in links_[i]:
                    if rest[j] < t + d:
                        rest[j] = t + d
            out.append(rest)
        return out

    def least(line_, a, b, old, rests):
        total, span = 0.0, line_[a:b + 1]
        inside, prev0, nxt = set(span), {}, {}
        for i in line_[a - 1::-1] if a else ():
            prev0.setdefault(queue[i], i)
            if len(prev0) == len(queues):
                break
        for i in line_[b + 1:]:
            nxt.setdefault(queue[i], i)
            if len(nxt) == len(queues):
                break
        for (cost_, late_, links_), (end, _), rest, out in zip(plans, old, rests, onward):
            free = {q: end[i] for q, i in prev0.items()}
            new, most = {}, 0.0
            for i in span:
                t = free.get(queue[i], 0.0)
                for j, d in links_[i]:
                    t = max(t, new.get(j, end[j]) + d)
                t = new[i] = free[queue[i]] = t + cost_[i]
                for k, d in out[i]:
                    if k not in inside:
                        most = max(most, t + d + rest[k])
            total += max([most] + [free[q] + rest[i] for q, i in nxt.items() if q in free])
        return total

    onward = [[[] for _ in ops] for _ in plans]
    for out, (_, _, links_) in zip(onward, plans):
        for i in range(n):
            for j, d in links_[i]:
                out[j].append((i, d))
    twins = {}
    for i, o in enumerate(ops):
        twins.setdefault(o["role"], []).append(i)
    blank = [([0.0] * n, [-1] * n) for _ in plans]
    best, state = play(line, 0, blank)
    for _ in range(TUNE["tries"]):
        new = list(rank_) if draw(100) >= TUNE["just"] else [-sum(r_) / len(plans) for r_ in zip(*tails(line))]
        for _ in range(draw(7)):
            i, d = draw(n), (draw(100) - 50) * TUNE["noise"] / 100
            for k in twins[ops[i]["role"]] if draw(2) else [i]:
                for j in [k] + (before[k] if d < 0 else after[k]):
                    new[j] += d
        i, patience = draw(n), list(look)
        patience[i:i + 60] = [draw(9) / 4] * len(look[i:i + 60])
        at = lay(new, patience)
        laid = sorted(range(n), key=lambda i: (at[i], i))
        total, tried = play(laid, 0, blank)
        if total <= best:
            best, state, line, rank_, look = total, tried, laid, new, patience
    found, now, keep, rests = waits(state), best, line, tails(line)
    for turn in range(TUNE["turns"]):
        p, i = found[draw(len(found))]
        a, b = line.index(p), line.index(i)
        early = draw(2)
        for _ in range(draw(3) if draw(4) else draw(16)):
            if early:
                a = next((k for k in range(a - 1, -1, -1) if queue[line[k]] == queue[i]), a)
            else:
                b = next((k for k in range(b + 1, n) if queue[line[k]] == queue[i]), b)
        span = line[a:b + 1]
        moved = {span[-1] if early else span[0]}
        for k in (span[-2::-1] if early else span[1:]):
            if any(j in moved for j in (after[k] if early else before[k])):
                moved.add(k)
        if len(moved) == len(span) or (span[0] if early else span[-1]) in moved:
            continue
        go, stay = [k for k in span if k in moved], [k for k in span if k not in moved]
        new = line[:a] + (go + stay if early else stay + go) + line[b + 1:]
        bound = now + TUNE["slack"] * (1 - turn / TUNE["turns"]) * draw(100) / 100
        if least(new, a, b, state, rests) > bound:
            continue
        total, tried = play(new, a, state)
        if total <= bound:
            now, state = total, tried
            line = sorted(new, key=lambda k: state[0][0][k] - cost[k])
            found, rests = waits(state), tails(line)
            if now < best:
                best, keep = now, line
    ORDER["end"] = best / len(plans)
    return keep


def rank_program(g, core, T, topo):
    rank = T.rank_of(core)
    if rank is None:
        return
    eng = {"V": g.vector, "S": g.scalar, "P": g.tensor, "G": g, "Y": g.sync}
    ops = []
    acc = {}
    ahead = [0.0]
    gate = []

    def v(name, a=0, b=None, s=1):
        buf, at, n = PLACE[name]
        a, b = at + a, at + (n if b is None else b)
        ap = T[buf][:, a:b] if s == 1 else T[buf][:, a:b:s]
        run_ = (a // 512 * 512, (b + 511) // 512 * 512, 1) if buf == "ps" else (a, b, s)
        return (ap, [(buf, run_)], len(range(a, b, s)), SIZE[SCRATCH[buf][2]], False)

    def w(name):
        return v(name, 0, C)

    def runs(n):
        return [(K * i // n, K * (i + 1) // n) for i in range(n)]

    def wd(name, p, a=0):
        return v(name, a + 16 * p[0], a + 16 * p[1])

    def sh(name, p):
        return v(name, p[0], p[1])

    def upto(name, p):
        return v(name, 0, 16 * p[1])

    def nth(name, j, p=(0, K)):
        return v(name, j + 16 * p[0], j + 16 * p[1] - 15, 16)

    def last(name, p=(0, K)):
        return nth(name, 15, p)

    def first(name, p=(0, K)):
        return nth(name, 0, p)

    def col(j, name="cols"):
        return v(name, j, j + 1)

    def ind(win, off):
        return (win[0].indirect(off[0]), win[1] + off[1], 16 * off[2], win[3], True)

    def bits(x, kind):
        return (x[0].bitcast(kind),) + x[1:]

    def add(q, issue, reads, writes, cost, late=0.0, sem=None, inc=1):
        need = set()
        for wr, rs in ((False, reads), (True, writes)):
            for name, run_ in rs:
                for a in acc.get(name, []):
                    if (wr or a[1] or (name == "ps" and a[2] != q)) and _meet(run_, a[0]):
                        need.add(a[3])
        me = len(ops)
        ops.append(dict(q=q, issue=issue, need=need, cost=cost, late=late, sem=sem or "q" + q, inc=inc, ahead=ahead[0],
                        behind={j for j in gate if ops[j]["q"] == q},
                        role=(q,) + tuple((name.rstrip("012"), r_) for name, r_ in writes[:1] + list(reads[:1]))))
        for name, r_ in writes:
            acc[name] = [a for a in acc.get(name, []) if not (
                r_[0] <= a[0][0] and a[0][1] <= r_[1] and (r_[2] == 1 or (r_[2] == a[0][2] and _meet(r_, a[0]))))]
            acc[name].append((r_, True, q, me))
        for name, r_ in reads:
            acc.setdefault(name, []).append((r_, False, q, me))

    def run(q, fn, out, args, cost, kw=None, more=(), reads=(), late=0.0):
        kw = kw or {}
        rd = [r for a in list(args) + list(kw.values()) + list(reads) if isinstance(a, tuple) for r in a[1]]
        wr = list(out[1]) + [r for a in more for r in a[1]]
        pick = lambda a: a[0] if isinstance(a, tuple) else a
        add(q, lambda: fn(out[0], *[a[0] for a in more], *[pick(a) for a in args], **{k: pick(a) for k, a in kw.items()}),
            rd, wr, cost, late)

    def plain(a, per):
        return ("g", 0.055, a[2]) if a[4] else ("c", 0.0, max(64, a[2] * per))

    def half(*xs):
        return 0.5 if all(x[3] == 2 for x in xs) else 1

    def tt(out, a, b, op):
        run("V", g.vector.tensor_tensor, out, [a, b, op],
            plain(a, 1) if a[4] or a[1][0][0] == "ps" or a[2] <= 32 else ("t", 0.0, a[2]))

    def ts(out, a, s1, op0, s2=None, op1=None):
        run("V", g.vector.tensor_scalar, out, [a, s1, s2, op0] + ([] if op1 is None else [op1]), plain(a, half(out, a)))

    def cp(out, a):
        run("V", g.vector.tensor_copy, out, [a], plain(a, half(out, a)))

    def turn(out, a):
        run("V", g.vector.transpose, out, [a], plain(a, half(out, a)))

    def scan(out, d0, d1, op0, op1):
        run("V", g.vector.tensor_tensor_scan, out, [d0, d1, 0.0, op0, op1], plain(out, half(out, d0, d1)))

    def total(out, d):
        scan(out, v("keep", 0, d[2]), d, Alu.mult, Alu.add)

    def fill(out, c):
        run("V", g.vector.memset, out, [c], plain(out, half(out)))

    def quant(q, s, a):
        run("V", g.vector.quantize_mx, q, [a], ("c", 0.012 + 0.00022 * a[2], 0), more=[s])

    def act(out, a, scale=1.0, bias=None, func=None):
        kw = {} if scale == 1.0 else {"scale": scale}
        if bias is not None:
            kw["bias"] = bias
        if func is None:
            func = Act.Copy if bias is None and not isinstance(scale, tuple) else Act.Identity
        run("S", g.scalar.activation, out, [a, func], plain(a, 1), kw)

    def times(q, out, a, c=1.0):
        if q == "S":
            act(out, a, c)
        elif q == "G":
            run("G", g.affine_select, out, [a, [[0, a[2]]], Alu.is_gt, 0.0, 1, 0], ("c", 0.2, 2 * a[2]))
        elif c == 1.0:
            cp(out, a)
        else:
            ts(out, a, c, Alu.mult)

    def gather(q, out, a, win, off, p):
        for h, e_ in zip(runs(2), q) if p == (0, K) and q[0] != q[1] else [(p, q[p[0] // (p[1] - p[0]) % len(q)])]:
            times(e_, wd(out, h, a), ind(win, sh(off, h)))

    def spread(q, out, hold, short, p, a, b, op):
        x = first(hold, p) if q == "V" else sh(short, p)
        tt(x, a, b, op)
        if q == "V":
            total(wd(out, p), wd(hold, p))
        else:
            act(wd(out, p), ind(v(short, 0, p[1]), sh("kk", p)))
        return x

    def bank(b, n=C):
        return v("ps", 512 * b, 512 * b + n)

    def mm(at, wq, ws, b, x, xs, a=0, n=C, start=True, stop=True):
        run("P", g.tensor.matmul_mx, bank(at, n),
            [v(wq, 128 * b, 128 * b + 128), v(ws, 128 * b, 128 * b + 128), v(x, a, a + n), v(xs, a, a + n), start, stop],
            ("p", 0.0, n + 16), late="psum")

    def iota(out, pattern, base=0, mult=0, small=True):
        run("G", g.iota, out, [pattern, base, mult], ("c", 0.15, 2 * out[2]),
            {"allow_small_or_imprecise_dtypes": True} if small else {})

    def load(q, sem, out, src, late, reads=()):
        add(q, lambda: eng[q].dma_start(out[0], src), reads, out[1], ("c", 0.05, 0), late, sem, 16)

    def store(q, dst, ap, reads):
        add(q, lambda: eng[q].dma_start(dst, ap), reads, [], ("c", 0.05, 0), 2.2, "stored", 16)

    def peer(r):
        return T.cores[rank ^ ROUNDS[r]]

    sent = [0]

    reach = [k for k in topo.engines(core, peer(0)) if all(k in topo.engines(core, peer(j)) for j in range(3))]

    def send(dst, land, src, sem, late, share):
        all_ = topo.engines(core, dst) if TUNE["wide"] else reach
        e_ = all_[len(all_) * share[0] // 4:len(all_) * share[1] // 4]
        rid, pid, _ = topo.addr(dst)
        sent[0] += len(e_)
        add("G", lambda: g.remote_dma(land[0], src[0], T.sem[sem], T.sem.sent, pid, rid, sum(1 << k for k in e_)),
            src[1], land[1], ("call", 0.0, 1), late, (sem,), len(e_))

    PM, CA, CB, ST, SN, I16, GL, E15B = range(8)
    GE6, E15, LT6, LT14, LT15 = col(6, "ge"), col(15, "ge"), col(6, "lt"), col(14, "lt"), col(15, "lt")
    cuts = [[(lo, hi, 4 * (i % 2)) for i, (lo, hi) in enumerate(zip((0,) + c, c + (C,)))] for c in TUNE["cut"]]

    load("Y", "dx", v("x0"), T.x[:], 3.7)
    load("S", "dpar", v("pari"), T.par[:], 2.1)
    load("S", "dnod", v("nodi"), T.nod[:], 2.1)
    load("S", "du", v("ut"), T.u[:], 2.6)
    load("Y", "dwc", bits(v("qw"), dt.uint8), T.wc[:], 4.0)
    load("Y", "dws", v("sw"), T.ws[:], 4.0)
    load("Y", "dv", v("vt"), T.v[:], 4.0)

    jt = w("jt")
    iota(v("pidx", 0, 1), [[0, 1]], 0, 1, False)
    fill(v("keep"), 1.0)
    fill(v("keep", 0, C + 16, 16), 0.0)
    total(v("jt"), v("keep"))
    iota(v("k16"), [[16, K]])
    iota(v("k256"), [[256, K]])
    iota(v("uli"), [[16, 2], [32, 4], [0, 2]])
    iota(v("iota", 0, C), [[1, C]])
    iota(v("valt"), [[1, 16], [0, 16]])
    iota(v("idn"), [[1, 128]], 0, -1)
    iota(v("valt2"), [[1, 256]])
    act(v("ktab"), v("valt2"), 512.0)
    iota(v("xtab"), [[8192, 16]])
    for name, c in (("spk", 0), ("rmp", -1), ("dtu", 1), ("dng", 1)):
        iota(v(name), [[0, C]], c)
    iota(v("wdec", 0, 2 * C + 2, 2), [[0, C + 1]], -1)
    act(v("iota", C, 2 * C), v("iota", 0, C), 1.0, float(C))
    ts(v("pidx", 1, 2), v("pidx", 0, 1), 15, Alu.bitwise_and)
    ts(v("pidx", 2, 3), v("pidx", 0, 1), 16, Alu.bitwise_and)
    cp(col(PM), v("pidx", 1, 2))
    ts(col(1, "half"), v("pidx", 2, 3), C / 16, Alu.mult)
    ts(v("ge"), v("jt", 0, 16), col(PM), Alu.is_le)
    ts(v("gc"), v("jt", 0, 16), col(PM), Alu.is_le, float(C), Alu.mult)
    ts(v("lt"), v("jt", 0, 16), col(PM), Alu.is_gt)
    act(col(I16), col(PM), 16.0)
    act(col(ST), LT15, 1024.0)
    act(col(GL), col(1, "lt"), 8192.0, -1024.0)
    act(v("jt16"), jt, 16.0)
    ts(v("diag"), v("jt"), col(PM), Alu.is_equal)
    act(v("ta"), v("diag"), -8192.0)
    act(v("tb"), v("diag"), -0.125)
    scan(v("selw", 0, C + 1), v("tb", 15, C + 16), v("ta", 0, C + 1), Alu.mult, Alu.add)
    act(v("selg"), v("selw", 1, C + 1))
    tt(last("selg"), last("selg"), v("k256"), Alu.add)
    ts(v("thr"), jt, col(PM), Alu.is_lt, -2.0 ** -110, Alu.mult)
    ts(v("tw2"), v("valt"), col(PM), Alu.is_equal)
    tt(v("tw2"), v("tw2"), v("diag", 0, 256), Alu.max)
    iota(last("dtu"), [[-16, K]], -128)
    iota(last("dng"), [[0, K]], -1)

    def middle_constants():
        act(col(SN), LT15, 1024.0, 15 * 8192.0)
        act(col(CA), LT15, 2.0, col(PM))
        act(col(CB), LT15, 1.0, 14.0)
        act(col(E15B), E15, 2000.0)
        ts(v("turn"), v("jt", 0, 16), 1.0, Alu.add, col(CA), Alu.is_equal)
        act(v("spc"), jt, 0.0)
        act(v("dse"), w("diag"), -1024.0)
        act(last("dse"), v("k16"), 0.0, -1024.0)
        ts(col(0, "half"), v("pidx", 2, 3), 0.0, Alu.is_equal)
        ts(col(2, "half"), v("pidx", 2, 3), 0.0, Alu.is_gt)
        unpackers("qd", "sd", 1.0)

    ts(v("idn"), v("idn"), 0.0, Alu.is_equal)
    fill(v("et", 0, 1024), 0.0)
    load("Y", "dz", v("et", 1024, 2048), T.et[:, 0:1024], 2.3, v("et", 0, 1024)[1])

    def unpackers(q, s, m):
        for b in range(4):
            act(v("et", 512 * b + b, 512 * (b + 1), 4), v("idn"), m)
            quant(v(q, 128 * b, 128 * b + 128), v(s, 128 * b, 128 * b + 128), v("et", 512 * b, 512 * (b + 1)))

    cp(v("ulu"), v("uli"))
    quant(v("qu"), v("su"), v("ut"))
    cp(bits(v("qur"), dt.uint32), ind(bits(v("qu"), dt.uint32), v("ulu")))
    act(v("sur"), ind(v("su"), v("ulu")))

    def glob(out, tmp, loc, off=None):
        tt(v(tmp), loc, v("k256"), Alu.add)
        if off is None:
            ts(v(out), v(tmp), 0.0625, Alu.mult)
        else:
            ts(v(out), v(tmp), off, Alu.subtract, 0.0625, Alu.mult)

    def diagonal(out, x):
        scan(out, v("selw", 0, x[2]), x, Alu.add, Alu.max)

    def places(out, tmp, x, p):
        scan(wd(tmp, p), wd(x, p), wd("selg", p), Alu.max, Alu.add)
        ts(sh(out, p), last(tmp, p), col(GL), Alu.add, 0.0625, Alu.mult)

    ahead[0] = 30.0
    cp(v("nodu"), v("nodi"))
    moves = []
    e = reach
    n = len(e) // 4
    for r in range(3):
        rid, pid, _ = topo.addr(peer(r))
        moves.append(RemoteDMATransfer(dst_ids=[DstId(rid=rid, pnc=pid)], remote_sem=T.sem["an%d" % r],
                                       dma_engine_mask=sum(1 << k for k in e[r * n:(r + 1) * n]),
                                       src=T.nodu[:], dst=T["np%d" % r][:]))
    sent[0] += 3 * n
    add("G", lambda: g.remote_dma_fused(moves, local_sem=T.sem.sent), v("nodu")[1],
        v("np0")[1] + v("np1")[1] + v("np2")[1], ("call", 0.0, 1), "first", ("an0", "an1", "an2"), n)
    ahead[0] = 0.0
    act(v("nodnr"), ind(v("iota", 0, C), v("nodu")))
    ts(v("noda"), v("nodi"), col(1, "half"), Alu.add)
    turn(v("s1"), v("nodnr"))
    for o in (0, 1):
        ts(v("nodb", o, K, 2), v("s1", 16 * o, C, 32), float(C * o), Alu.add)

    def late_constants():
        for p in runs(2):
            run("V", g.vector.tensor_copy, (ind(v("inv1"), sh("nodu", p))[0], v("inv1")[1]), [wd("iota", p)],
                ("g", 0.05, C), reads=[v("nodu"), v("inv1")] if p[0] else [v("nodu")])
        for p in runs(2):
            diagonal(wd("inv2", p), wd("inv1", p))
        if min(TUNE["packed"]) == 0:
            ts(v("inv0"), last("inv2"), col(ST), Alu.subtract)
        if max(TUNE["packed"]):
            for o in (0, 1):
                ts(v("invu", o, 2 * K, 2), last("inv2"), col(ST), Alu.subtract)
            unpackers("qde", "sde", col(0, "half"))
            unpackers("qdo", "sdo", col(2, "half"))
        quant(v("qv"), v("sv"), v("vt"))

    ts(v("g0"), v("pari"), 16.0, Alu.mult, col(PM), Alu.add)
    ts(first("spk"), v("pari"), col(I16), Alu.add)
    ts(v("t1"), v("pari"), col(PM), Alu.subtract, 0.0, Alu.max)
    cp(v("t2"), v("pari"))
    tt(v("t0"), v("t2"), v("k16"), Alu.add)
    for p in runs(TUNE["td"][0]):
        total(wd("nbk", p), wd("spk", p))
        tt(wd("cmk", p), ind(v("valt2"), sh("g0", p)), wd("nbk", p), Alu.is_equal)
        total(wd("pos", p), wd("cmk", p))
        tt(sh("t1", p), sh("t1", p), last("pos", p), Alu.mult)
        tt(sh("link", p), sh("t0", p), sh("t1", p), Alu.subtract)
        tt(sh("t2", p), sh("t2", p), sh("t1", p), Alu.subtract)
        cp(sh("g1", p), sh("link", p))
        ts(sh("d2u", p), sh("t2", p), 16.0, Alu.mult, col(PM), Alu.add)
        times(TUNE["early"][0] if p[0] else "S", wd("pa", p), ind(v("jt16"), sh("g1", p)))
    gate[:] = [len(ops) - 3]
    quant(v("qb0", 0, C), v("sb0", 0, C), v("x0"))
    gate[:] = []

    for r in range(3):
        to = peer(r)
        final, parts, packed = r == 2, cuts[r], TUNE["packed"][r]
        qb, sb, lx, ls, qe, se, qo, so, og, ol, ws, wl, nw = (
            n + str(r) for n in ("qb", "sb", "lx", "ls", "qe", "se", "qo", "so", "og", "ol", "ws", "wl", "nw"))
        send(to, bits(v(lx), dt.uint8), bits(v(qb, 0, C), dt.uint8), "ax%d" % r, "big" if r else "first", TUNE["ex"])
        send(to, v(ls), v(sb, 0, C), "as%d" % r, "big" if r else "first", TUNE["es"])
        for p in runs(TUNE["td"][r > 0]):
            times("S" if r or not p[0] else TUNE["early"][1], wd("pb", p), ind(upto("pa", p), sh("g1", p)))
            act(wd("d2", p), ind(v("tw2"), sh("d2u", p)), 2.0, -1.0)
            times(TUNE["copy"][2 * (r > 0)], wd("c2", p), wd("d2", p))
            places("g2", "h2", "pb", p)
            act(wd("pc", p), ind(upto("pb", p), sh("g2", p)))
            tt(wd("d4", p), ind(upto("d2", p), sh("g2", p)), wd("c2", p), Alu.max)
            times(TUNE["copy"][2 * (r > 0) + 1], wd("c4", p), wd("d4", p))
            places("g4", "h4", "pc", p)
            tt(wd("d8", p), ind(upto("d4", p), sh("g4", p)), wd("c4", p), Alu.max)
        if r == 0:
            gate[:] = [len(ops) - 4, len(ops) - 1]
            middle_constants()
            gate[:] = []
        for i, (lo, hi, _) in enumerate(cuts[r - 1] if r else [(0, C, 0)]):
            for o in (0, 1):
                mm(2 * i + o, "qur", "sur", o, qb, sb, lo, hi - lo)
                times(TUNE["sc"][2 * i + o], v("sc", C * o + lo, C * o + hi), bank(2 * i + o, hi - lo))
        for p in runs(TUNE["t1"]):
            gather(TUNE["f1"], "f1", 0, v("sc"), "nodb", p)
        gate_ = [len(ops) - 1] if r and TUNE["late8"] else []
        for p in runs(TUNE["td"][r > 0]):
            gate[:] = gate_ if p[0] or TUNE["late8"] > 1 else []
            act(wd("c8", p), ind(upto("d8", p), sh("g4", p)))
            gate[:] = []
            tt(wd("db", p), ind(upto("c8", p), sh("g4", p)), wd("d8", p), Alu.max)
            total(wd("siz", p), wd("db", p))
        for p in runs(TUNE["t1"]):
            turn(wd("f2", p), wd("f1", p))
            tt(wd("dif", p), ind(v("sc"), sh("noda", p)), wd("f2", p), Alu.subtract)
            tt(wd("cmpm", p), wd("dif", p), wd("thr", p), Alu.is_gt)
            total(wd("stsc", p), wd("cmpm", p))
            ts(sh("stu", p), last("stsc", p), 0.0, Alu.add)
        act(v("stc"), last("stsc"), 1.0, -16.5)
        act(first("rmp"), last("stsc"), 1.0, -0.5)
        gate_ = []
        for p in runs(TUNE["t2"]):
            both = (2 * p[0], 2 * p[1])
            low, high = (2 * p[0], p[0] + p[1]), (p[0] + p[1], 2 * p[1])
            act(sh("sab", low), last("siz", p), 256.0, 4096.0)
            act(sh("sab", high), last("siz", p), -256.0, 4096.0)
            if r == 0:
                ts(sh("ends", low), sh("k256", p), col(I16), Alu.add, col(ST), Alu.add)
                act(sh("ends", high), sh("link", p), 16.0, col(ST))
            act(wd("stn", p), ind(v("jt", 0, 16), sh("stu", p)))
            tt(wd("xx", p), ind(v("xtab"), sh("stu", p)), wd("db", p), Alu.mult)
            scan(wd("mx", low), wd("keep", p), wd("xx", p), Alu.mult, Alu.max)
            scan(wd("mx", high), wd("xx", p), wd("dng", p), Alu.min, Alu.mult)
            tt(sh("far", both), last("mx", both), sh("sab", both), Alu.add)
            tt(first("spk", p), sh("far", low), sh("far", high), Alu.min)
            total(wd("nbk", p), wd("spk", p))
            ts(sh("keyu", p), first("spk", p), 2.0 ** -9, Alu.mult)
            tt(wd("cmk", p), ind(v("ktab"), sh("keyu", p)), wd("nbk", p), Alu.is_lt)
            total(wd("pos", p), wd("cmk", p))
            ts(sh("posu", p), last("pos", p), 0.0, Alu.add)
            tt(sh("near", both), last("mx", both), sh("ends", both), Alu.add)
            tt(sh("vm", p), sh("near", low), sh("near", high), Alu.max)
            ts(sh("o3u", p), sh("vm", p), col(SN), Alu.subtract, 0.0625, Alu.mult)
            act(wd("stl", p), ind(upto("stn", p), sh("o3u", p)))
            tt(wd("g3c", p), ind(v("turn"), sh("posu", p)), wd("stl", p), Alu.mult)
            total(wd("wc1", p), wd("g3c", p))
            ts(sh(ws, p), last("wc1", p), GE6, Alu.mult, col(CB), Alu.min)
            gate_.append(len(ops) - 1)
        send(to, v(wl), v(ws), "aw%d" % r, "word", TUNE["ew"])
        gate_.append(len(ops) - 1)
        gate[:] = gate_[-1:] if TUNE["free"] else gate_
        tt(v("oh"), ind(v("diag", 0, 16), v("stu")), v("iota", 0, C), Alu.mult)
        total(v("osum"), v("oh"))
        ts(v(og), last("osum"), 0.0, Alu.add)
        send(to, v(ol), v(og), "ao%d" % r, "word", TUNE["eo"])
        gate[:] = gate_
        if r == 0:
            late_constants()
        total(v("rs"), v("rmp"))
        ts(v("wdec", 1, 2 * C, 2), v("rs"), -1.0, Alu.max, 0.0, Alu.min)
        act(v("srcw", 0, C), ind(v("nodnr"), v(og)))
        act(v("won"), ind(v("jt16"), v(og)))
        act(v(nw), ind(v("iota", C, 2 * C), v("np%d" % r)))
        act(v("srcw", C, 2 * C), ind(v(nw), v(ol)))
        act(v("ownm"), last("wc1"), LT6)
        tt(v("owng"), v("ownm"), v("k16"), Alu.add)
        for b in range(4):
            mm(4 + b, "qd", "sd", b, lx, ls)
            times(TUNE["ft"][b], v("ft", b, 4 * C, 4), bank(4 + b))
        quant(v(qb, C, 2 * C), v(sb, C, 2 * C), v("ft"))
        gate[:] = []
        for b in range(packed, 4):
            mm(b, "qd", "sd", b, qb, sb)
            act(v("wt%d" % b, 0, C), bank(b), 0.5)
            if TUNE["twice"]:
                act(v("fh%d" % b), bank(b), 0.5)
            else:
                load("Y", "dh%d" % b, v("fh%d" % b), v("wt%d" % b, 0, C)[0], 3.0, v("wt%d" % b, 0, C)[1])
            mm(4 + b, "qd", "sd", b, qb, sb, C)
            act(v("wt%d" % b, C, 2 * C), bank(4 + b), 0.5)
        for p in runs(TUNE["t4"]):
            at = 16 * (p[0] // (p[1] - p[0]))
            cg = first("spc", p)
            tt(cg, sh(wl, p), sh("owng", p), Alu.add)
            total(wd("nbc", p), wd("spc", p))
            ts(sh("cgu", p), cg, 0.0, Alu.add)
            act(nth("dse", 14, p), cg, 2.0, LT14)
            ts(sh("sju", p), cg, col(6, "gc"), Alu.add, col(14, "gc"), Alu.subtract)
            tt(wd("eq", p), ind(v("iota", 0, C), sh("cgu", p)), wd("nbc", p), Alu.is_equal)
            scan(wd("seen", p), wd("eq", p), wd("dse", p), Alu.max, Alu.add)
            ts(sh("of2", p), nth("seen", 14, p), col(E15B), Alu.max, 2.0 * C, Alu.min)
            gather(TUNE["ab"], "ab", at + 1, v("wdec", 0, 2 * C + 1), "of2", p)
            total(wd("asum", p), wd("ab", p, at + 1))
            tt(nth("ab", at, p), sh("stc", p), last("asum", p), Alu.subtract)
            scan(wd("yq", p), wd("thr", p), wd("ab", p, at), Alu.max, Alu.add)
            ts(wd("hh", p), wd("yq", p), -0.5, Alu.is_equal, 113.0, Alu.mult)
            scan(wd("trn", p), wd("hh", p), wd("dtu", p), Alu.max, Alu.add)
            ts(sh("tu", p), last("trn", p), -1.0, Alu.mult)
            act(wd("sj", p), ind(v("srcw"), sh("sju", p)))
            gather(TUNE["sn"], "sn", 0, upto("sj", p), "tu", p)
        act(v("lj"), ind(v("won"), v("cgu")))
        if not final:
            act(last("lj"), last("won"))
        for i, (lo, hi, _) in enumerate([] if packed else parts):
            times(TUNE["cw"][i], v("cw", lo, hi), ind(v("sn"), v("inv0", lo // 16, hi // 16)))
            gate_ = [len(ops) - 1]
            diagonal(v("dm", lo, hi), v("cw", lo, hi))
            ts(v("mine", lo // 16, hi // 16), v("dm", lo + 15, hi, 16), col(ST), Alu.subtract)
        for i, (lo, hi, _) in enumerate(parts if packed else []):
            times(TUNE["cw"][i], v("cw", 2 * lo, 2 * hi), ind(v("sn"), v("invu", lo // 8, hi // 8)))
            gate_ = [len(ops) - 1]
            turn(v("dl", 2 * lo, 2 * hi), v("cw", 2 * lo, 2 * hi))
            for o in (0, 1):
                ts(v("pick", 32 * o + lo // 16, 32 * o + hi // 16), v("dl", 2 * lo + 16 * o, 2 * hi, 32), 0.0, Alu.add)
            if packed < 4:
                diagonal(v("dm", 2 * lo, 2 * hi), v("cw", 2 * lo, 2 * hi))
                ts(v("mine", lo // 16, hi // 16), v("dm", 2 * lo + 15, 2 * hi, 32), col(ST), Alu.subtract)
        if final:
            act(v("opn"), ind(v("lj"), v("tu")), 0.0625)
            store("Y", T.op[:], T.opn[0:128:16, :], v("opn")[1])
        for p in [] if final else runs(TUNE["td"][1]):
            gate[:] = gate_ if p[0] or TUNE["double"] else []
            act(wd("pa", p), ind(upto("lj", p), sh("tu", p)))
            gate[:] = []
            diagonal(wd("lsc", p), wd("pa", p))
            ts(sh("d2u", p), last("lsc", p), col(ST), Alu.subtract, col(PM), Alu.add)
            link = sh("ends", (p[0] + p[1], 2 * p[1]))
            tt(link, last("lsc", p), sh("k256", p), Alu.add)
            ts(sh("g1", p), link, col(ST), Alu.subtract, 0.0625, Alu.mult)
        ahead[0] = 0.0
        gate_ = []
        nq, ns = ("qx", "sx") if final else ("qb%d" % (r + 1), "sb%d" % (r + 1))
        for lo, hi, at in parts:
            n = hi - lo
            for b in range(packed):
                mm(at + b, "qd", "sd", b, qb, sb, lo, n, True, False)
            for q, s, o, e_, es in ((qe, se, 0, "qde", "sde"), (qo, so, 32, "qdo", "sdo")) if packed else ():
                gate[:] = gate_
                off = v("pick", o + lo // 16, o + hi // 16)
                cp(bits(v(q, lo, hi), dt.uint32), ind(bits(v(qb), dt.uint32), off))
                act(v(s, lo, hi), ind(v(sb), off))
                gate_ = [len(ops) - 2, len(ops) - 1]
                for b in range(packed):
                    mm(at + b, e_, es, b, q, s, lo, n, False, o > 0)
                    gate_.append(len(ops) - 1)
                gate[:] = []
            for b in range(packed):
                times(TUNE["z"][final][at + b], v("zt", 4 * lo + b, 4 * hi, 4), bank(at + b, n), 0.5)
            for b in range(packed, 4):
                tt(v("zt", 4 * lo + b, 4 * hi, 4), ind(v("wt%d" % b), v("mine", lo // 16, hi // 16)),
                   v("fh%d" % b, lo, hi), Alu.add)
            quant(v("qz", lo, hi), v("sz", lo, hi), v("zt", 4 * lo, 4 * hi))
            if TUNE["whole"]:
                times("V", v("z32", 4 * lo, 4 * hi), v("zt", 4 * lo, 4 * hi), 32.0)
            for b in range(4):
                at4 = (4 * lo + b, 4 * hi, 4)
                if not TUNE["whole"]:
                    times(TUNE["z32"][final][at + b], v("z32", *at4), v("zt", *at4), 32.0)
                mm(at + b, "qw", "sw", b, "qz", "sz", lo, n)
                tt(v("x32", *at4), bank(at + b, n), v("z32", *at4), Alu.add)
                times(TUNE["xs"][final][at + b], v("xt", *at4), v("x32", *at4), 0.03125)
            quant(v(nq, lo, hi), v(ns, lo, hi), v("xt", 4 * lo, 4 * hi))

    for i, (lo, hi, at) in enumerate(parts):
        mm(at, "qv", "sv", 0, "qx", "sx", lo, hi - lo)
        times("SV"[i % 2], v("yt", lo, hi), bank(at, hi - lo))
        store("SY"[i % 2], T.y[:, lo:hi], T.yt[:, lo:hi], v("yt", lo, hi)[1])
        store("Y", T.oc[:, 4 * lo:4 * hi], T.qx[:, lo:hi].bitcast(dt.uint8), v("qx", lo, hi)[1])
    for k in range(4):
        store("SY"[k % 2], T.osc[4 * k:4 * k + 4, :], T.sx[32 * k:32 * k + 4, :], v("sx")[1])

    if "line" not in ORDER:
        ORDER["line"] = _order(ops, list(eng))
    count = {s: 0 for s in SEMAPHORES}
    known = {q: {} for q in eng}
    token = {}

    def wait(q, marks, knew):
        k = known[q]
        for s, c in marks:
            if k.get(s, 0) < c:
                eng[q].wait_ge(T.sem[s], c)
                for s2, c2 in list(knew.items()) + [(s, c)]:
                    if k.get(s2, 0) < c2:
                        k[s2] = c2

    for i in ORDER["line"]:
        o = ops[i]
        q = o["q"]
        for j in sorted(o["need"], key=lambda j: -token[j][2]):
            if not (q == "P" and ops[j]["q"] == "P"):
                wait(q, token[j][0], token[j][1])
        ins = o["issue"]()
        if isinstance(o["sem"], tuple):
            for s in o["sem"]:
                count[s] += o["inc"]
            token[i] = ([(s, count[s]) for s in o["sem"]], {}, len(token))
        else:
            count[o["sem"]] += o["inc"]
            ins.then_inc(T.sem[o["sem"]], o["inc"])
            token[i] = ([(o["sem"], count[o["sem"]])], dict(known[q]), len(token))
    count["sent"] = sent[0]
    for s in SEMAPHORES:
        if count[s]:
            wait("G", [(s, count[s])], {})
